import numpy as np
import ml_dtypes


def mxq(x, axis, fmt="e4m3"):
    dtype, down = {"e4m3": (ml_dtypes.float8_e4m3fn, 7), "e5m2": (ml_dtypes.float8_e5m2, 14)}[fmt]
    v = np.moveaxis(np.asarray(x, np.float32).astype(ml_dtypes.bfloat16).astype(np.float64), axis, -1)
    blocks = v.reshape(v.shape[:-1] + (-1, 32))
    amax = np.abs(blocks).max(-1, keepdims=True)
    byte = np.maximum(np.where(amax > 0, np.frexp(amax)[1] - 1 + 127, 0) - down, 1)
    scale = np.exp2(byte - 127.0)
    codes = (blocks / scale).astype(np.float32).astype(dtype).astype(np.float64)
    return np.moveaxis((codes * scale).reshape(v.shape), -1, axis)


WIDE = False


def mx_kscale(k):
    if not WIDE:
        return np.ones(k)
    levels = np.array([10, -10, 5, -5, 0])
    if k % 512:
        return np.exp2(np.random.permutation(np.resize(levels, k // 32))).repeat(32)
    a = np.empty((k // 512, 16))
    for p in range(k // 512):
        a[p, :8] = np.random.permutation(np.resize(levels, 8))
        for g in range(8):
            far = levels[np.abs(levels - a[p, g]) >= 10]
            a[p, g + 8] = far[np.random.randint(len(far))]
    return np.exp2(a.ravel()).repeat(32)


def f64(x):
    return np.asarray(x).astype(np.float64)


def striped(idx):
    return np.tile(idx.reshape(-1, 16).T, (8, 1)).astype(np.uint16)


def unstriped(offs):
    return offs[:16].T.reshape(-1).astype(np.int64)


E2M1 = np.array([0.0, 0.5, 1.0, 1.5, 2.0, 3.0, 4.0, 6.0, -0.0, -0.5, -1.0, -1.5, -2.0, -3.0, -4.0, -6.0])


def pack_weight(w, fmt):
    k, n = w.shape
    w = f64(np.asarray(w, np.float32).astype(ml_dtypes.bfloat16)).reshape(k // 32, 32, n)
    amax = np.abs(w).max(1)
    if fmt == "e4m3":
        byte = np.frexp(amax)[1] - 1 + 127 - 7
    else:
        mant, ex = np.frexp(amax / 6.0)
        byte = np.where(mant > 0.5, ex, ex - 1) + 127
    byte = np.clip(np.where(amax > 0, byte, 1), 1, 254)
    scaled = (w * np.exp2(127.0 - byte)[:, None, :]).reshape(k, n).astype(np.float32)
    by_word = np.ascontiguousarray(scaled.reshape(k // 512, 128, 4, n).transpose(0, 1, 3, 2))
    if fmt == "e4m3":
        words = by_word.astype(ml_dtypes.float8_e4m3fn).view(np.uint8)
    else:
        c = by_word.astype(ml_dtypes.float4_e2m1fn).view(np.uint8) & 0xF
        words = (c[..., 0::2] | (c[..., 1::2] << 4)).reshape(k // 512, 128, 2 * n)
    return np.ascontiguousarray(words), np.ascontiguousarray(byte.astype(np.uint8).reshape(k // 512, 16, n))


def unpack_weight(words, scales, fmt):
    g, _, n = scales.shape
    words = np.ascontiguousarray(words).reshape(g, 128, n, -1)
    if fmt == "e4m3":
        vals = words.view(ml_dtypes.float8_e4m3fn).astype(np.float64)
    else:
        nib = np.empty((g, 128, n, 4), np.uint8)
        nib[..., 0::2] = words & 0xF
        nib[..., 1::2] = words >> 4
        vals = E2M1[nib]
    vals = vals * np.repeat(np.exp2(scales.astype(np.float64) - 127.0), 8, axis=1)[..., None]
    return vals.transpose(0, 1, 3, 2).reshape(g * 512, n)


def gelu(v):
    return 0.5 * v * (1.0 + np.tanh(np.sqrt(2.0 / np.pi) * (v + 0.044715 * v**3)))


K, T, S, H, N = 1024, 2048, 1024, 512, 384

def setup_inputs():
    n = np.random.standard_normal
    s = mx_kscale(K)[:, None]
    u = mx_kscale(H)[:, None]
    tab_words, tab_scales = pack_weight(n((K, T)) * s, "e4m3")
    wt_words, wt_scales = pack_weight(n((K, H)) / np.sqrt(K) / s, "e2m1")
    return {
        "tab_words": tab_words, "tab_scales": tab_scales,
        "offs": striped(np.random.permutation(T)[:S]),
        "offs2": striped(np.random.permutation(T)[:S]),
        "offs3": striped(np.random.permutation(T)[:S]),
        "wp": (n((K, H)) / np.sqrt(K) / s).astype(np.float32),
        "wt_words": wt_words, "wt_scales": wt_scales,
        "wr": (n((K, H)) / np.sqrt(K) / s).astype(np.float32),
        "g": (np.exp(0.3 * n(H)) * u[:, 0]).astype(np.float32),
        "wo": (2.0 * n((H, N)) / np.sqrt(H) / u).astype(np.float32),
    }

def reference(tab_words, tab_scales, offs, offs2, offs3, wp, wt_words, wt_scales, wr, g, wo):
    vp = unpack_weight(tab_words, tab_scales, "e4m3")[:, unstriped(offs)]
    vt = unpack_weight(tab_words, tab_scales, "e4m3")[:, unstriped(offs2)]
    vr = unpack_weight(tab_words, tab_scales, "e4m3")[:, unstriped(offs3)]
    wt = unpack_weight(wt_words, wt_scales, "e2m1")
    p = mxq(f64(wp), 0, "e4m3").T @ vp
    c = wt.T @ vt + mxq(f64(wr), 0, "e4m3").T @ vr
    gate = 1.0 / (1.0 + np.exp(-p))
    h = gate * np.tanh(c) * f64(g)[:, None]
    y = mxq(f64(wo), 0, "e4m3").T @ mxq(h, 0, "e4m3")
    return np.tanh(y)

@@ -1,0 +1,252 @@
+from contextlib import ExitStack
+
+import concourse.mybir as mybir
+
+K, T, S, H, N = 1024, 2048, 1024, 512, 384
+FLOPS = 2 * S * (3 * K * H + H * N)
+
+F32 = mybir.dt.float32
+BF16 = mybir.dt.bfloat16
+I32 = mybir.dt.int32
+U32 = mybir.dt.uint32
+U16 = mybir.dt.uint16
+U8 = mybir.dt.uint8
+FP8X4 = mybir.dt.float8_e4m3fn_x4
+FP4X4 = mybir.dt.float4_e2m1fn_x4
+ACT = mybir.ActivationFunctionType
+MULT = mybir.AluOpType.mult
+
+P = 128
+PASSES = K // 512
+HALF = 512
+UNIT = 128
+SLOT = 10240
+HELD = ("wp_raw0", "wp_raw1", "wr_raw0", "wr_raw1", "wt_raw", "wo_raw", "gain", "tab", "tab_second_pass")
+REUSED = {
+    (1, 0, 0): ("wt_raw", 0), (1, 1, 0): ("wt_raw", 1), (2, 0, 0): ("wt_raw", 2),
+    (2, 1, 0): ("wr_raw1", 0), (1, 0, 1): ("wr_raw1", 1), (1, 1, 1): ("wr_raw1", 2), (2, 0, 1): ("wr_raw1", 3),
+    (2, 1, 1): ("wr_raw1", 4),
+}
+CHUNKS = (256, 256, 256, 128, 128)
+
+
+def tile_list_paged_memory_cell_kernel(
+    tc, tab_words, tab_scales, offs, offs2, offs3, wp, wt_words, wt_scales, wr, g, wo, out
+):
+    nc = tc.nc
+    with ExitStack() as ctx:
+        keep = ctx.enter_context(tc.tile_pool(name="keep", bufs=1))
+        psum = ctx.enter_context(tc.psum_pool(name="psum", bufs=8))
+
+        front = ctx.enter_context(tc.tile_pool(name="front", bufs=1))
+
+        def tile(name, shape, dtype):
+            return keep.tile(shape, dtype, name=name, align_bytes=64)
+
+        def held(name, shape, dtype, slot=None, at=0):
+            return front.tile(shape, dtype, name=name, offset=HELD.index(slot or name) * SLOT + at, align_bytes=64)
+
+        zeros = front.tile([P, len(HELD) * SLOT // 4], I32, name="zeros", offset=0, align_bytes=64)
+
+        tab_sc = tile("tab_sc", [P, T], U8)
+        wt_sc_raw = tile("wt_sc_raw", [P, PASSES * H], U8)
+        tok_sc1 = tile("tok_sc1", [P, S], U8)
+        nc.gpsimd.memset(tab_sc[:].bitcast(I32), 0)
+        nc.vector.memset(zeros[:, : PASSES * H // 4], 0)
+        nc.vector.tensor_copy(out=wt_sc_raw[:].bitcast(I32), in_=zeros[:, : PASSES * H // 4])
+        nc.gpsimd.memset(tok_sc1[:].bitcast(I32), 0)
+
+        lists = []
+        for name, src in (("page", offs), ("token", offs2), ("pred", offs3)):
+            lst = tile("list_" + name, [P, S // 16], U16)
+            nc.sync.dma_start(lst[:], src)
+            lists.append(lst)
+        for q in range(4):
+            nc.sync.dma_start(
+                out=tab_sc[32 * q : 32 * q + 8, :].bitcast(I32),
+                in_=tab_scales[:, 4 * q : 4 * q + 4, :].bitcast(I32),
+            )
+
+        def load_rows(name, w, a):
+            raw = (held if name in HELD else tile)(name, [P, SLOT // 4], F32)
+            rows = raw[:, : 4 * H].rearrange("p (j r) -> p j r", j=4)
+            nc.sync.dma_start(out=rows, in_=w[512 * a : 512 * (a + 1), :].rearrange("(p j) r -> p j r", j=4))
+            return rows
+
+        wp_raw = [load_rows("wp_raw0", wp, 0)]
+        tab = held("tab", [P, PASSES * T], I32)
+        nc.sync.dma_start(
+            out=tab[:].rearrange("p (a t) -> p a t", a=PASSES),
+            in_=tab_words.rearrange("a p t i -> p a (t i)").bitcast(I32),
+        )
+        wp_raw.append(load_rows("wp_raw1", wp, 1))
+        wr_raw = [load_rows("wr_raw0", wr, 0)]
+        wt_slot = held("wt_raw", [P, SLOT // 4], I32)
+        wt_raw = wt_slot[:, : PASSES * H // 2].rearrange("p (a w) -> p a w", a=PASSES)
+        nc.sync.dma_start(out=wt_raw, in_=wt_words.bitcast(I32).rearrange("a p w -> p a w"))
+        for q in range(4):
+            nc.sync.dma_start(
+                out=wt_sc_raw[32 * q : 32 * q + 4, :].bitcast(I32).rearrange("r (a w) -> r a w", a=PASSES),
+                in_=wt_scales[:, 4 * q : 4 * q + 4, :].bitcast(I32).rearrange("a r w -> r a w"),
+            )
+        wr_raw.append(load_rows("wr_raw1", wr, 1))
+        gain = [held("gain%d" % t, [P, 1], F32, "gain", 64 * t) for t in range(4)]
+        g_rows = g.rearrange("(c t i o) -> t c i o", t=4, i=4, o=1)
+        with nc.allow_non_contiguous_dma(reason="one gain value for each partition"):
+            for t in range(4):
+                nc.sync.dma_start(out=gain[t][:], in_=g_rows[t])
+        wo_raw = held("wo_raw", [P, 4, N], F32)
+        wo_rows = wo.rearrange("(c t i) n -> t c i n", t=4, i=4)
+        for t in range(4):
+            nc.sync.dma_start(out=wo_raw[:, t, :], in_=wo_rows[t])
+
+        def gather_scales(n):
+            picked = tile("picked_sc%d" % n, [P, S], U8)
+            nc.vector.tensor_copy(picked[:], tab_sc[:].indirect(lists[n][:]))
+            return picked
+
+        def gather_words(n, a, half):
+            name = "picked%d_%d_%d" % (n, a, half)
+            if n == 0:
+                picked = tile(name, [P, HALF], U32)
+            else:
+                slot, place = REUSED[(n, a, half)]
+                picked = held(name, [P, HALF], U32, slot, 4 * HALF * place)
+            cols = slice(half * HALF // 16, (half + 1) * HALF // 16)
+            nc.vector.tensor_copy(picked[:], tab[:, a * T : (a + 1) * T].bitcast(U32).indirect(lists[n][:, cols]))
+            return picked
+
+        def round_weight(name, raw):
+            grouped = tile(name, [P, 4 * H], BF16)
+            nc.scalar.copy(
+                out=grouped[:].rearrange("p (t c i j) -> p t c j i", t=4, i=4, j=4),
+                in_=raw.rearrange("p j (c t i) -> p t c j i", t=4, i=4),
+            )
+            return grouped
+
+        def quantize(name, grouped, width):
+            codes = tile(name + "_codes", [P, width], U32)
+            scales = tile(name + "_scales", [P, width], U8)
+            nc.vector.quantize_mx(out=codes[:].bitcast(FP8X4), scales=scales[:], in_=grouped)
+            return codes, scales
+
+        wp_bf = [round_weight("wp_bf%d" % a, wp_raw[a]) for a in range(PASSES)]
+        wr_bf = [round_weight("wr_bf%d" % a, wr_raw[a]) for a in range(PASSES)]
+        picked_sc = [gather_scales(n) for n in range(3)]
+        nc.gpsimd.dma_start(out=tok_sc1[0:100, :].bitcast(I32), in_=picked_sc[1][4:104, :].bitcast(I32))
+        wp_q = [quantize("wp%d" % a, wp_bf[a][:], H) for a in range(PASSES)]
+        wr_q = [quantize("wr%d" % a, wr_bf[a][:], H) for a in range(PASSES)]
+
+        def fp8_pass(bank, t, weight, n, a, picked, half, start, stop):
+            codes, scales = weight
+            m = slice(P * t, P * (t + 1))
+            nc.tensor.matmul_mx(
+                out=bank[:],
+                lhsT=codes[:, m].bitcast(FP8X4),
+                lhsT_scale=scales[:, m],
+                rhs=picked[:].bitcast(FP8X4),
+                rhs_scale=picked_sc[n][4 * a : P, half * HALF : (half + 1) * HALF],
+                start=start,
+                stop=stop,
+            )
+
+        gated = []
+        for half in range(2):
+            banks = [psum.tile([P, HALF], F32, name="bank") for t in range(4)]
+            for a in range(PASSES):
+                picked = gather_words(0, a, half)
+                for t in range(4):
+                    fp8_pass(banks[t], t, wp_q[a], 0, a, picked, half, a == 0, a == PASSES - 1)
+            sig = tile("sig%d" % half, [P, 4, HALF], F32)
+            gate = tile("gate%d" % half, [P, 4, HALF], F32)
+            for t in range(4):
+                nc.scalar.activation(out=sig[:, t, :], in_=banks[t][:], func=ACT.Sigmoid)
+            for t in range(4):
+                nc.vector.tensor_scalar(
+                    out=gate[:, t, :], in0=sig[:, t, :], scalar1=gain[t][:], scalar2=None, op0=MULT
+                )
+            gated.append(gate)
+
+        wt_codes = tile("wt_codes", [P, PASSES * H // 2], I32)
+        wt_sc = tile("wt_sc", [P, PASSES * H // 4], I32)
+        nc.vector.tensor_copy(
+            out=wt_codes[:].rearrange("p (a t c w) -> p a t c w", a=PASSES, t=4, w=2),
+            in_=wt_raw.rearrange("p a (c t w) -> p a t c w", t=4, w=2),
+        )
+        nc.vector.tensor_copy(
+            out=wt_sc[:].rearrange("p (a t c) -> p a t c", a=PASSES, t=4),
+            in_=wt_sc_raw[:].bitcast(I32).rearrange("p (a c t) -> p a t c", a=PASSES, t=4),
+        )
+
+        cells = []
+        for half in range(2):
+            banks = [psum.tile([P, HALF], F32, name="bank") for t in range(4)]
+            cols = slice(half * HALF, (half + 1) * HALF)
+            for a in range(PASSES):
+                picked = gather_words(1, a, half)
+                for t in range(4):
+                    w0 = (4 * a + t) * (P // 2)
+                    s0 = (4 * a + t) * (P // 4)
+                    nc.tensor.matmul_mx(
+                        out=banks[t][:],
+                        lhsT=wt_codes[:, w0 : w0 + P // 2].bitcast(FP4X4),
+                        lhsT_scale=wt_sc[:, s0 : s0 + P // 4].bitcast(U8),
+                        rhs=picked[:].bitcast(FP8X4),
+                        rhs_scale=(picked_sc[1], tok_sc1)[a][:, cols],
+                        start=a == 0,
+                        stop=False,
+                    )
+            for a in range(PASSES):
+                picked = gather_words(2, a, half)
+                for t in range(4):
+                    fp8_pass(banks[t], t, wr_q[a], 2, a, picked, half, False, a == PASSES - 1)
+            for quarter in range(2):
+                cell = tile("cell%d_%d" % (half, quarter), [P, 4, HALF // 2], F32)
+                for t in range(4):
+                    nc.scalar.activation(
+                        out=cell[:, t, :], in_=banks[t][:, quarter * 256 : (quarter + 1) * 256], func=ACT.Tanh
+                    )
+                cells.append(cell)
+
+        wo_bf = tile("wo_bf", [P, 4 * N], BF16)
+        nc.scalar.copy(
+            out=wo_bf[:].rearrange("p (c i t) -> p c t i", t=4, i=4),
+            in_=wo_raw[:].rearrange("p t (c i) -> p c t i", i=4),
+        )
+        wo_q = [quantize("wo_a", wo_bf[:, : 4 * 256], 256), quantize("wo_b", wo_bf[:, 4 * 256 :], 128)]
+        wo_tiles = [(wo_q[0], 0), (wo_q[0], P), (wo_q[1], 0)]
+
+        out_rows = out.rearrange("(nt p) s -> p nt s", p=P)
+        s0 = 0
+        for width in CHUNKS:
+            h_bf = tile("h_bf%d" % s0, [P, 4 * width], BF16)
+            gate = gated[s0 // HALF][:, :, s0 % HALF : s0 % HALF + width]
+            cell = cells[s0 // 256][:, :, s0 % 256 : s0 % 256 + width]
+            nc.vector.tensor_tensor(
+                out=h_bf[:].rearrange("p (c i t) -> p c t i", t=4, i=4),
+                in0=gate.rearrange("p t (c i) -> p c t i", i=4),
+                in1=cell.rearrange("p t (c i) -> p c t i", i=4),
+                op=MULT,
+            )
+            h_codes, h_scales = quantize("h%d" % s0, h_bf[:], width)
+            state = tile("state%d" % s0, [P, 3, width], F32)
+            for u0 in range(0, width, UNIT):
+                bank = psum.tile([P, HALF], F32, name="bank")
+                for nt in range(3):
+                    (codes, scales), m0 = wo_tiles[nt]
+                    nc.tensor.matmul_mx(
+                        out=bank[:, nt * UNIT : (nt + 1) * UNIT],
+                        lhsT=codes[:, m0 : m0 + P].bitcast(FP8X4),
+                        lhsT_scale=scales[:, m0 : m0 + P],
+                        rhs=h_codes[:, u0 : u0 + UNIT].bitcast(FP8X4),
+                        rhs_scale=h_scales[:, u0 : u0 + UNIT],
+                        start=True,
+                        stop=True,
+                    )
+                nc.scalar.activation(
+                    out=state[:, :, u0 : u0 + UNIT],
+                    in_=bank[:, : 3 * UNIT].rearrange("p (nt s) -> p nt s", nt=3),
+                    func=ACT.Tanh,
+                )
+            nc.sync.dma_start(out=out_rows[:, :, s0 : s0 + width], in_=state[:])
+            s0 = s0 + width

@@ -15,6 +15,7 @@ FP8X4 = mybir.dt.float8_e4m3fn_x4
 FP4X4 = mybir.dt.float4_e2m1fn_x4
 ACT = mybir.ActivationFunctionType
 MULT = mybir.AluOpType.mult
+ADD = mybir.AluOpType.add
 
 P = 128
 PASSES = K // 512
@@ -162,8 +163,8 @@ def tile_list_paged_memory_cell_kernel(
             for t in range(4):
                 nc.scalar.activation(out=sig[:, t, :], in_=banks[t][:], func=ACT.Sigmoid)
             for t in range(4):
-                nc.vector.tensor_scalar(
-                    out=gate[:, t, :], in0=sig[:, t, :], scalar1=gain[t][:], scalar2=None, op0=MULT
+                nc.gpsimd.tensor_scalar(
+                    out=gate[:, t, :], in0=sig[:, t, :], scalar1=gain[t][:], scalar2=0.0, op0=MULT, op1=ADD
                 )
             gated.append(gate)
 

@@ -21,12 +21,13 @@ P = 128
 PASSES = K // 512
 HALF = 512
 UNIT = 128
-SLOT = 10240
-HELD = ("wp_raw0", "wp_raw1", "wr_raw0", "wr_raw1", "wt_raw", "wo_raw", "gain", "tab", "tab_second_pass")
+SLOT = 8192
+HELD = ("wp_raw0", "wp_raw1", "wr_raw0", "wr_raw1", "wt_raw", "wo_raw", "gain", "tab", "tab_second_pass", "wr_bf0", "wr_bf1")
 REUSED = {
-    (1, 0, 0): ("wt_raw", 0), (1, 1, 0): ("wt_raw", 1), (2, 0, 0): ("wt_raw", 2),
-    (2, 1, 0): ("wr_raw1", 0), (1, 0, 1): ("wr_raw1", 1), (1, 1, 1): ("wr_raw1", 2), (2, 0, 1): ("wr_raw1", 3),
-    (2, 1, 1): ("wr_raw1", 4),
+    (0, 1, 1): ("wp_raw1", 0),
+    (1, 0, 0): ("wt_raw", 0), (1, 1, 0): ("wt_raw", 1),
+    (2, 0, 0): ("wr_bf0", 0), (1, 0, 1): ("wr_bf0", 1),
+    (2, 1, 0): ("wr_bf1", 0), (1, 1, 1): ("wr_bf1", 1), (2, 0, 1): ("wr_bf1", 2), (2, 1, 1): ("wr_bf1", 3),
 }
 CHUNKS = (256, 256, 256, 128, 128)
 
@@ -108,7 +109,7 @@ def tile_list_paged_memory_cell_kernel(
 
         def gather_words(n, a, half):
             name = "picked%d_%d_%d" % (n, a, half)
-            if n == 0:
+            if (n, a, half) not in REUSED:
                 picked = tile(name, [P, HALF], U32)
             else:
                 slot, place = REUSED[(n, a, half)]
@@ -118,15 +119,19 @@ def tile_list_paged_memory_cell_kernel(
             return picked
 
         def round_weight(name, raw):
-            grouped = tile(name, [P, 4 * H], BF16)
+            grouped = (held if name in HELD else tile)(name, [P, SLOT // 2], BF16)[:, : 4 * H]
             nc.scalar.copy(
-                out=grouped[:].rearrange("p (t c i j) -> p t c j i", t=4, i=4, j=4),
+                out=grouped.rearrange("p (t c i j) -> p t c j i", t=4, i=4, j=4),
                 in_=raw.rearrange("p j (c t i) -> p t c j i", t=4, i=4),
             )
             return grouped
 
         def quantize(name, grouped, width):
-            codes = tile(name + "_codes", [P, width], U32)
+            if name == "h0":
+                slot, place = REUSED[(2, 1, 1)]
+                codes = held(name + "_codes", [P, width], U32, slot, 4 * HALF * place)
+            else:
+                codes = tile(name + "_codes", [P, width], U32)
             scales = tile(name + "_scales", [P, width], U8)
             nc.vector.quantize_mx(out=codes[:].bitcast(FP8X4), scales=scales[:], in_=grouped)
             return codes, scales
@@ -135,8 +140,8 @@ def tile_list_paged_memory_cell_kernel(
         wr_bf = [round_weight("wr_bf%d" % a, wr_raw[a]) for a in range(PASSES)]
         picked_sc = [gather_scales(n) for n in range(3)]
         nc.gpsimd.dma_start(out=tok_sc1[0:100, :].bitcast(I32), in_=picked_sc[1][4:104, :].bitcast(I32))
-        wp_q = [quantize("wp%d" % a, wp_bf[a][:], H) for a in range(PASSES)]
-        wr_q = [quantize("wr%d" % a, wr_bf[a][:], H) for a in range(PASSES)]
+        wp_q = [quantize("wp%d" % a, wp_bf[a], H) for a in range(PASSES)]
+        wr_q = [quantize("wr%d" % a, wr_bf[a], H) for a in range(PASSES)]
 
         def fp8_pass(bank, t, weight, n, a, picked, half, start, stop):
             codes, scales = weight
@@ -158,7 +163,7 @@ def tile_list_paged_memory_cell_kernel(
                 picked = gather_words(0, a, half)
                 for t in range(4):
                     fp8_pass(banks[t], t, wp_q[a], 0, a, picked, half, a == 0, a == PASSES - 1)
-            sig = tile("sig%d" % half, [P, 4, HALF], F32)
+            sig = held("sig%d" % half, [P, 4, HALF], F32, ("wr_raw0", "wr_raw1")[half])
             gate = tile("gate%d" % half, [P, 4, HALF], F32)
             for t in range(4):
                 nc.scalar.activation(out=sig[:, t, :], in_=banks[t][:], func=ACT.Sigmoid)

@@ -58,6 +58,10 @@ def tile_list_paged_memory_cell_kernel(
         nc.vector.tensor_copy(out=wt_sc_raw[:].bitcast(I32), in_=zeros[:, : PASSES * H // 4])
         nc.gpsimd.memset(tok_sc1[:].bitcast(I32), 0)
 
+        warm = tile("warm", [P, 2], F32)
+        nc.gpsimd.memset(warm[:, 0:1], 0.0)
+        nc.scalar.activation(out=warm[:, 1:2], in_=warm[:, 0:1], func=ACT.Sigmoid)
+
         lists = []
         for name, src in (("page", offs), ("token", offs2), ("pred", offs3)):
             lst = tile("list_" + name, [P, S // 16], U16)

@@ -172,7 +172,7 @@ def tile_list_paged_memory_cell_kernel(
             for t in range(4):
                 nc.scalar.activation(out=sig[:, t, :], in_=banks[t][:], func=ACT.Sigmoid)
             for t in range(4):
-                nc.gpsimd.tensor_scalar(
+                nc.vector.tensor_scalar(
                     out=gate[:, t, :], in0=sig[:, t, :], scalar1=gain[t][:], scalar2=0.0, op0=MULT, op1=ADD
                 )
             gated.append(gate)

@@ -20,16 +20,13 @@ ADD = mybir.AluOpType.add
 P = 128
 PASSES = K // 512
 HALF = 512
+CHUNK = 256
 UNIT = 128
-SLOT = 8192
-HELD = ("wp_raw0", "wp_raw1", "wr_raw0", "wr_raw1", "wt_raw", "wo_raw", "gain", "tab", "tab_second_pass", "wr_bf0", "wr_bf1")
-REUSED = {
-    (0, 1, 1): ("wp_raw1", 0),
-    (1, 0, 0): ("wt_raw", 0), (1, 1, 0): ("wt_raw", 1),
-    (2, 0, 0): ("wr_bf0", 0), (1, 0, 1): ("wr_bf0", 1),
-    (2, 1, 0): ("wr_bf1", 0), (1, 1, 1): ("wr_bf1", 1), (2, 0, 1): ("wr_bf1", 2), (2, 1, 1): ("wr_bf1", 3),
-}
-CHUNKS = (256, 256, 256, 128, 128)
+PAGE, TOKEN, PRED = 0, 1, 2
+SLOTS = {"wp1": 0, "page": 4096, "wr0": 4096 + 2048, "wr1": 14336 + 2048, "wo": 26624, "h0": 26624 + 3072, "h1": 26624 + 3072,
+         "cell0": 32768, "gate1": 32768}
+LOAD = 8192
+LOADS = ("wt_raw", "wp_raw0", "wp_raw1", "tab0", "tab1", "wr_raw0", "wr_raw1", "wo_raw", "gain")
 
 
 def tile_list_paged_memory_cell_kernel(
@@ -38,225 +35,282 @@ def tile_list_paged_memory_cell_kernel(
     nc = tc.nc
     with ExitStack() as ctx:
         keep = ctx.enter_context(tc.tile_pool(name="keep", bufs=1))
-        psum = ctx.enter_context(tc.psum_pool(name="psum", bufs=8))
+        shared = ctx.enter_context(tc.tile_pool(name="shared", bufs=1))
+        psum = ctx.enter_context(tc.psum_pool(name="psum", bufs=1))
 
         front = ctx.enter_context(tc.tile_pool(name="front", bufs=1))
 
-        def tile(name, shape, dtype):
-            return keep.tile(shape, dtype, name=name, align_bytes=64)
+        def tile(name, shape, dtype, slot=None, at=0):
+            if name in LOADS or slot in LOADS:
+                return front.tile(shape, dtype, name=name, offset=LOADS.index(slot or name) * LOAD + at, align_bytes=64)
+            if slot not in SLOTS:
+                return keep.tile(shape, dtype, name=name, align_bytes=64)
+            return shared.tile(shape, dtype, name=name, offset=SLOTS[slot] + at, align_bytes=64)
 
-        def held(name, shape, dtype, slot=None, at=0):
-            return front.tile(shape, dtype, name=name, offset=HELD.index(slot or name) * SLOT + at, align_bytes=64)
-
-        zeros = front.tile([P, len(HELD) * SLOT // 4], I32, name="zeros", offset=0, align_bytes=64)
+        def bank(b):
+            return psum.tile([P, 512], F32, name="bank%d" % b)
 
         tab_sc = tile("tab_sc", [P, T], U8)
+        nc.gpsimd.memset(tab_sc[:].bitcast(I32), 0)
+        zeros = front.tile([P, len(LOADS) * LOAD // 4], I32, name="zeros", offset=0, align_bytes=64)
         wt_sc_raw = tile("wt_sc_raw", [P, PASSES * H], U8)
         tok_sc1 = tile("tok_sc1", [P, S], U8)
-        nc.gpsimd.memset(tab_sc[:].bitcast(I32), 0)
+        warm = tile("warm", [P, 2], F32)
+        nc.vector.memset(warm[:, 0:1], 0.0)
         nc.vector.memset(zeros[:, : PASSES * H // 4], 0)
         nc.vector.tensor_copy(out=wt_sc_raw[:].bitcast(I32), in_=zeros[:, : PASSES * H // 4])
         nc.gpsimd.memset(tok_sc1[:].bitcast(I32), 0)
-
-        warm = tile("warm", [P, 2], F32)
-        nc.gpsimd.memset(warm[:, 0:1], 0.0)
         nc.scalar.activation(out=warm[:, 1:2], in_=warm[:, 0:1], func=ACT.Sigmoid)
 
-        lists = []
-        for name, src in (("page", offs), ("token", offs2), ("pred", offs3)):
-            lst = tile("list_" + name, [P, S // 16], U16)
+        def load_list(name, src):
+            lst = tile(name, [P, S // 16], U16)
             nc.sync.dma_start(lst[:], src)
-            lists.append(lst)
+            return lst
+
+        def load_table(a):
+            words = tile("tab%d" % a, [P, T], I32)
+            nc.sync.dma_start(out=words[:], in_=tab_words[a].rearrange("p t i -> p (t i)").bitcast(I32))
+            return words
+
+        def load_rows(name, w, a):
+            rows = tile(name, [P, 4, H], F32)
+            nc.sync.dma_start(out=rows[:], in_=w[512 * a : 512 * (a + 1), :].rearrange("(p j) r -> p j r", j=4))
+            return rows
+
+        lists = [load_list(name, src) for name, src in (("page", offs), ("token", offs2), ("pred", offs3))]
         for q in range(4):
             nc.sync.dma_start(
                 out=tab_sc[32 * q : 32 * q + 8, :].bitcast(I32),
                 in_=tab_scales[:, 4 * q : 4 * q + 4, :].bitcast(I32),
             )
-
-        def load_rows(name, w, a):
-            raw = (held if name in HELD else tile)(name, [P, SLOT // 4], F32)
-            rows = raw[:, : 4 * H].rearrange("p (j r) -> p j r", j=4)
-            nc.sync.dma_start(out=rows, in_=w[512 * a : 512 * (a + 1), :].rearrange("(p j) r -> p j r", j=4))
-            return rows
-
         wp_raw = [load_rows("wp_raw0", wp, 0)]
-        tab = held("tab", [P, PASSES * T], I32)
-        nc.sync.dma_start(
-            out=tab[:].rearrange("p (a t) -> p a t", a=PASSES),
-            in_=tab_words.rearrange("a p t i -> p a (t i)").bitcast(I32),
-        )
+        wt_raw = tile("wt_raw", [P, PASSES, H // 2], I32)
+        nc.sync.dma_start(out=wt_raw[:], in_=wt_words.bitcast(I32).rearrange("a p w -> p a w"))
         wp_raw.append(load_rows("wp_raw1", wp, 1))
-        wr_raw = [load_rows("wr_raw0", wr, 0)]
-        wt_slot = held("wt_raw", [P, SLOT // 4], I32)
-        wt_raw = wt_slot[:, : PASSES * H // 2].rearrange("p (a w) -> p a w", a=PASSES)
-        nc.sync.dma_start(out=wt_raw, in_=wt_words.bitcast(I32).rearrange("a p w -> p a w"))
+        tab = [load_table(0)]
         for q in range(4):
             nc.sync.dma_start(
                 out=wt_sc_raw[32 * q : 32 * q + 4, :].bitcast(I32).rearrange("r (a w) -> r a w", a=PASSES),
                 in_=wt_scales[:, 4 * q : 4 * q + 4, :].bitcast(I32).rearrange("a r w -> r a w"),
             )
-        wr_raw.append(load_rows("wr_raw1", wr, 1))
-        gain = [held("gain%d" % t, [P, 1], F32, "gain", 64 * t) for t in range(4)]
+        tab.append(load_table(1))
+        wr_raw = [load_rows("wr_raw0", wr, 0)]
+        gain = [tile("gain%d" % t, [P, 1], F32, "gain", 64 * t) for t in range(4)]
         g_rows = g.rearrange("(c t i o) -> t c i o", t=4, i=4, o=1)
         with nc.allow_non_contiguous_dma(reason="one gain value for each partition"):
             for t in range(4):
                 nc.sync.dma_start(out=gain[t][:], in_=g_rows[t])
-        wo_raw = held("wo_raw", [P, 4, N], F32)
+        wr_raw.append(load_rows("wr_raw1", wr, 1))
+        wo_raw = tile("wo_raw", [P, 4, N], F32)
         wo_rows = wo.rearrange("(c t i) n -> t c i n", t=4, i=4)
         for t in range(4):
             nc.sync.dma_start(out=wo_raw[:, t, :], in_=wo_rows[t])
 
-        def gather_scales(n):
-            picked = tile("picked_sc%d" % n, [P, S], U8)
-            nc.vector.tensor_copy(picked[:], tab_sc[:].indirect(lists[n][:]))
+        def gather(name, window, n, s0, count, dtype, slot=None, at=0):
+            picked = tile(name, [P, count], dtype, slot, at)
+            nc.vector.tensor_copy(picked[:], window.indirect(lists[n][:, s0 // 16 : (s0 + count) // 16]))
             return picked
 
-        def gather_words(n, a, half):
-            name = "picked%d_%d_%d" % (n, a, half)
-            if (n, a, half) not in REUSED:
-                picked = tile(name, [P, HALF], U32)
-            else:
-                slot, place = REUSED[(n, a, half)]
-                picked = held(name, [P, HALF], U32, slot, 4 * HALF * place)
-            cols = slice(half * HALF // 16, (half + 1) * HALF // 16)
-            nc.vector.tensor_copy(picked[:], tab[:, a * T : (a + 1) * T].bitcast(U32).indirect(lists[n][:, cols]))
-            return picked
+        def gather_scales(n, s0, count, slot=None, at=0):
+            return gather("sc%d_%d" % (n, s0), tab_sc[:], n, s0, count, U8, slot, at)
 
-        def round_weight(name, raw):
-            grouped = (held if name in HELD else tile)(name, [P, SLOT // 2], BF16)[:, : 4 * H]
-            nc.scalar.copy(
-                out=grouped.rearrange("p (t c i j) -> p t c j i", t=4, i=4, j=4),
-                in_=raw.rearrange("p j (c t i) -> p t c j i", t=4, i=4),
-            )
+        def gather_words(n, a, s0, count, slot=None, at=0):
+            return gather("w%d_%d_%d" % (n, a, s0), tab[a][:].bitcast(U32), n, s0, count, U32, slot, at)
+
+        def round_weight(name, raw, on_scalar):
+            grouped = tile(name + "_bf", [P, 4 * H], BF16, name)
+            dst = grouped[:].rearrange("p (t c i j) -> p t c j i", t=4, i=4, j=4)
+            src = raw[:].rearrange("p j (c t i) -> p t c j i", t=4, i=4)
+            if on_scalar:
+                nc.scalar.copy(out=dst[:, :on_scalar], in_=src[:, :on_scalar])
+            for t in range(on_scalar, 4):
+                nc.gpsimd.tensor_scalar(
+                    out=grouped[:, H * t : H * (t + 1)].rearrange("p (c i j) -> p c i j", i=4, j=4),
+                    in0=raw[:].rearrange("p j (c t i) -> p t c i j", t=4, i=4)[:, t],
+                    scalar1=1.0, scalar2=0.0, op0=MULT, op1=ADD,
+                )
             return grouped
 
         def quantize(name, grouped, width):
-            if name == "h0":
-                slot, place = REUSED[(2, 1, 1)]
-                codes = held(name + "_codes", [P, width], U32, slot, 4 * HALF * place)
-            else:
-                codes = tile(name + "_codes", [P, width], U32)
+            codes = tile(name + "_codes", [P, width], U32)
             scales = tile(name + "_scales", [P, width], U8)
             nc.vector.quantize_mx(out=codes[:].bitcast(FP8X4), scales=scales[:], in_=grouped)
             return codes, scales
 
-        wp_bf = [round_weight("wp_bf%d" % a, wp_raw[a]) for a in range(PASSES)]
-        wr_bf = [round_weight("wr_bf%d" % a, wr_raw[a]) for a in range(PASSES)]
-        picked_sc = [gather_scales(n) for n in range(3)]
-        nc.gpsimd.dma_start(out=tok_sc1[0:100, :].bitcast(I32), in_=picked_sc[1][4:104, :].bitcast(I32))
-        wp_q = [quantize("wp%d" % a, wp_bf[a], H) for a in range(PASSES)]
-        wr_q = [quantize("wr%d" % a, wr_bf[a], H) for a in range(PASSES)]
-
-        def fp8_pass(bank, t, weight, n, a, picked, half, start, stop):
-            codes, scales = weight
+        def fp8_pass(dst, t, weight, words, scales, start, stop):
             m = slice(P * t, P * (t + 1))
             nc.tensor.matmul_mx(
-                out=bank[:],
-                lhsT=codes[:, m].bitcast(FP8X4),
-                lhsT_scale=scales[:, m],
-                rhs=picked[:].bitcast(FP8X4),
-                rhs_scale=picked_sc[n][4 * a : P, half * HALF : (half + 1) * HALF],
+                out=dst,
+                lhsT=weight[0][:, m].bitcast(FP8X4),
+                lhsT_scale=weight[1][:, m],
+                rhs=words.bitcast(FP8X4),
+                rhs_scale=scales,
                 start=start,
                 stop=stop,
             )
 
-        gated = []
-        for half in range(2):
-            banks = [psum.tile([P, HALF], F32, name="bank") for t in range(4)]
-            for a in range(PASSES):
-                picked = gather_words(0, a, half)
-                for t in range(4):
-                    fp8_pass(banks[t], t, wp_q[a], 0, a, picked, half, a == 0, a == PASSES - 1)
-            sig = held("sig%d" % half, [P, 4, HALF], F32, ("wr_raw0", "wr_raw1")[half])
-            gate = tile("gate%d" % half, [P, 4, HALF], F32)
-            for t in range(4):
-                nc.scalar.activation(out=sig[:, t, :], in_=banks[t][:], func=ACT.Sigmoid)
-            for t in range(4):
-                nc.vector.tensor_scalar(
-                    out=gate[:, t, :], in0=sig[:, t, :], scalar1=gain[t][:], scalar2=0.0, op0=MULT, op1=ADD
-                )
-            gated.append(gate)
-
         wt_codes = tile("wt_codes", [P, PASSES * H // 2], I32)
         wt_sc = tile("wt_sc", [P, PASSES * H // 4], I32)
-        nc.vector.tensor_copy(
+        nc.gpsimd.tensor_copy(
             out=wt_codes[:].rearrange("p (a t c w) -> p a t c w", a=PASSES, t=4, w=2),
-            in_=wt_raw.rearrange("p a (c t w) -> p a t c w", t=4, w=2),
+            in_=wt_raw[:].rearrange("p a (c t w) -> p a t c w", t=4, w=2),
         )
-        nc.vector.tensor_copy(
+        nc.gpsimd.tensor_copy(
             out=wt_sc[:].rearrange("p (a t c) -> p a t c", a=PASSES, t=4),
             in_=wt_sc_raw[:].bitcast(I32).rearrange("p (a c t) -> p a t c", a=PASSES, t=4),
         )
 
-        cells = []
-        for half in range(2):
-            banks = [psum.tile([P, HALF], F32, name="bank") for t in range(4)]
+        words = {}
+        gates = []
+        wp_bf = [round_weight("wp%d" % a, wp_raw[a], 4) for a in range(PASSES)]
+
+        def page_half(half):
+            banks = [bank(4 * half + t) for t in range(4)]
             cols = slice(half * HALF, (half + 1) * HALF)
             for a in range(PASSES):
-                picked = gather_words(1, a, half)
                 for t in range(4):
-                    w0 = (4 * a + t) * (P // 2)
-                    s0 = (4 * a + t) * (P // 4)
-                    nc.tensor.matmul_mx(
-                        out=banks[t][:],
-                        lhsT=wt_codes[:, w0 : w0 + P // 2].bitcast(FP4X4),
-                        lhsT_scale=wt_sc[:, s0 : s0 + P // 4].bitcast(U8),
-                        rhs=picked[:].bitcast(FP8X4),
-                        rhs_scale=(picked_sc[1], tok_sc1)[a][:, cols],
-                        start=a == 0,
-                        stop=False,
-                    )
-            for a in range(PASSES):
-                picked = gather_words(2, a, half)
-                for t in range(4):
-                    fp8_pass(banks[t], t, wr_q[a], 2, a, picked, half, False, a == PASSES - 1)
-            for quarter in range(2):
-                cell = tile("cell%d_%d" % (half, quarter), [P, 4, HALF // 2], F32)
-                for t in range(4):
-                    nc.scalar.activation(
-                        out=cell[:, t, :], in_=banks[t][:, quarter * 256 : (quarter + 1) * 256], func=ACT.Tanh
-                    )
-                cells.append(cell)
+                    fp8_pass(banks[t][:], t, wp_q[a], words[PAGE, a, half], page_sc[4 * a : P, cols], a == 0, a == 1)
+            sig = tile("sig%d" % half, [P, 4, HALF], F32, "wr_raw%d" % half)
+            gate = tile("gate%d" % half, [P, 4, HALF], F32, "gate%d" % half)
+            for t in range(4):
+                nc.scalar.activation(out=sig[:, t, :], in_=banks[t][:], func=ACT.Sigmoid)
+            for t in range(4):
+                nc.gpsimd.tensor_scalar(
+                    out=gate[:, t, :], in0=sig[:, t, :], scalar1=gain[t][:], scalar2=0.0, op0=MULT, op1=ADD
+                )
+            gates.extend([gate[:, :, :CHUNK], gate[:, :, CHUNK:]])
 
-        wo_bf = tile("wo_bf", [P, 4 * N], BF16)
-        nc.scalar.copy(
-            out=wo_bf[:].rearrange("p (c i t) -> p c t i", t=4, i=4),
-            in_=wo_raw[:].rearrange("p t (c i) -> p c t i", i=4),
-        )
-        wo_q = [quantize("wo_a", wo_bf[:, : 4 * 256], 256), quantize("wo_b", wo_bf[:, 4 * 256 :], 128)]
-        wo_tiles = [(wo_q[0], 0), (wo_q[0], P), (wo_q[1], 0)]
+        def gather_group(name, keys, slot, at=0):
+            group = tile(name, [P, len(keys) * CHUNK], U32, slot, at)
+            for place, (n, a, q) in enumerate(keys):
+                dst = group[:, place * CHUNK : (place + 1) * CHUNK]
+                cols = slice(q * CHUNK // 16, (q + 1) * CHUNK // 16)
+                nc.vector.tensor_copy(dst, tab[a][:].bitcast(U32).indirect(lists[n][:, cols]))
+                words[n, a, q] = dst
+
+        def cell_chunk(q, by_unit):
+            banks = [bank(2 * (q % 2) + j) for j in range(2)]
+            passes = []
+            for a in range(PASSES):
+                for u in range(2):
+                    for t in range(4):
+                        passes.append((TOKEN, a, t, u * UNIT, UNIT))
+            for a in range(PASSES):
+                for u in range(2 if by_unit else 1):
+                    for t in range(4):
+                        passes.append((PRED, a, t, u * UNIT, UNIT if by_unit else CHUNK))
+            places = [(s0 // UNIT, t * UNIT) if by_unit else (t // 2, (t % 2) * CHUNK + s0) for n, a, t, s0, w in passes]
+            which = [b for b, c in places]
+            for k, (n, a, t, s0, width) in enumerate(passes):
+                b, col = places[k]
+                start = b not in which[:k]
+                stop = b not in which[k + 1 :]
+                dst = banks[b][:, col : col + width]
+                moving = words[n, a, q][:, s0 : s0 + width]
+                j0 = q * CHUNK + s0
+                if n == PRED:
+                    scales = pred_sc[j0 // HALF][4 * a : P, j0 % HALF : j0 % HALF + width]
+                    fp8_pass(dst, t, wr_q[a], moving, scales, start, stop)
+                else:
+                    w0 = (4 * a + t) * (P // 2)
+                    c0 = (4 * a + t) * (P // 4)
+                    nc.tensor.matmul_mx(
+                        out=dst,
+                        lhsT=wt_codes[:, w0 : w0 + P // 2].bitcast(FP4X4),
+                        lhsT_scale=wt_sc[:, c0 : c0 + P // 4].bitcast(U8),
+                        rhs=moving.bitcast(FP8X4),
+                        rhs_scale=(tok_sc0, tok_sc1)[a][:, j0 : j0 + width],
+                        start=start,
+                        stop=stop,
+                    )
+            cell = tile("cell%d" % q, [P, 2 * 512], F32, "cell%d" % q)
+            for b in range(2):
+                nc.scalar.activation(out=cell[:, 512 * b : 512 * (b + 1)], in_=banks[b][:], func=ACT.Tanh)
+            return cell
+
+        def product_on_gpsimd(q, cells):
+            h_bf = tile("h%d_bf" % q, [P, 4 * CHUNK], BF16, "h%d" % q)
+            for s0 in range(0, CHUNK, UNIT):
+                nc.gpsimd.tensor_tensor(
+                    out=h_bf[:, 4 * s0 : 4 * (s0 + UNIT)].rearrange("p (s t) -> p s t", t=4),
+                    in0=gates[q][:, :, s0 : s0 + UNIT].rearrange("p t s -> p s t"),
+                    in1=cells[:].rearrange("p (t s) -> p s t", t=4)[:, s0 : s0 + UNIT],
+                    op=MULT,
+                )
+            return h_bf
 
         out_rows = out.rearrange("(nt p) s -> p nt s", p=P)
-        s0 = 0
-        for width in CHUNKS:
-            h_bf = tile("h_bf%d" % s0, [P, 4 * width], BF16)
-            gate = gated[s0 // HALF][:, :, s0 % HALF : s0 % HALF + width]
-            cell = cells[s0 // 256][:, :, s0 % 256 : s0 % 256 + width]
-            nc.vector.tensor_tensor(
-                out=h_bf[:].rearrange("p (c i t) -> p c t i", t=4, i=4),
-                in0=gate.rearrange("p t (c i) -> p c t i", i=4),
-                in1=cell.rearrange("p t (c i) -> p c t i", i=4),
-                op=MULT,
-            )
-            h_codes, h_scales = quantize("h%d" % s0, h_bf[:], width)
+
+        def project(s0, width, h_q, first_bank):
             state = tile("state%d" % s0, [P, 3, width], F32)
             for u0 in range(0, width, UNIT):
-                bank = psum.tile([P, HALF], F32, name="bank")
+                dst = bank(first_bank + u0 // UNIT)
                 for nt in range(3):
                     (codes, scales), m0 = wo_tiles[nt]
                     nc.tensor.matmul_mx(
-                        out=bank[:, nt * UNIT : (nt + 1) * UNIT],
+                        out=dst[:, nt * UNIT : (nt + 1) * UNIT],
                         lhsT=codes[:, m0 : m0 + P].bitcast(FP8X4),
                         lhsT_scale=scales[:, m0 : m0 + P],
-                        rhs=h_codes[:, u0 : u0 + UNIT].bitcast(FP8X4),
-                        rhs_scale=h_scales[:, u0 : u0 + UNIT],
+                        rhs=h_q[0][:, u0 : u0 + UNIT].bitcast(FP8X4),
+                        rhs_scale=h_q[1][:, u0 : u0 + UNIT],
                         start=True,
                         stop=True,
                     )
                 nc.scalar.activation(
                     out=state[:, :, u0 : u0 + UNIT],
-                    in_=bank[:, : 3 * UNIT].rearrange("p (nt s) -> p nt s", nt=3),
+                    in_=dst[:, : 3 * UNIT].rearrange("p (nt s) -> p nt s", nt=3),
                     func=ACT.Tanh,
                 )
             nc.sync.dma_start(out=out_rows[:, :, s0 : s0 + width], in_=state[:])
-            s0 = s0 + width
+
+        def product_on_vector(name, gate, cell, width):
+            h_bf = tile(name + "_bf", [P, 4 * width], BF16, name)
+            nc.vector.tensor_tensor(
+                out=h_bf[:].rearrange("p (c i t) -> p c t i", t=4, i=4),
+                in0=gate.rearrange("p t (c i) -> p c t i", i=4),
+                in1=cell.rearrange("p (t c i) -> p c t i", t=4, i=4),
+                op=MULT,
+            )
+            return h_bf
+
+        tok_sc0 = gather_scales(TOKEN, 0, S)
+        nc.gpsimd.dma_start(out=tok_sc1[0:100, :].bitcast(I32), in_=tok_sc0[4:104, :].bitcast(I32))
+        page_sc = gather_scales(PAGE, 0, S)
+        pred_all = gather_scales(PRED, 0, S)
+        pred_sc = [pred_all[:, :HALF], pred_all[:, HALF:]]
+        wp_q = [quantize("wp%d" % a, wp_bf[a][:], H) for a in range(PASSES)]
+        wr_bf = [round_weight("wr0", wr_raw[0], 3), round_weight("wr1", wr_raw[1], 2)]
+        words[PAGE, 0, 0] = gather_words(PAGE, 0, 0, HALF)[:]
+        gather_group("chunk0_a", [(TOKEN, 0, 0), (PRED, 0, 0), (TOKEN, 0, 1)], "wp1")
+        words[PAGE, 1, 0] = gather_words(PAGE, 1, 0, HALF)[:]
+        page_half(0)
+        gather_group("chunk0_b", [(TOKEN, 1, 0), (PRED, 1, 0)], "none")
+        wr_q = [quantize("wr0", wr_bf[0][:], H)]
+        words[PAGE, 0, 1] = gather_words(PAGE, 0, HALF, HALF, "wr0", 0)[:]
+        gather_group("early1", [(TOKEN, 1, 1), (PRED, 0, 1)], "wr0", 2048)
+        wr_q.append(quantize("wr1", wr_bf[1][:], H))
+        wo_bf = tile("wo_bf", [P, 4 * N], BF16, "wo")
+        for n0, n1 in ((0, 256), (256, N)):
+            nc.scalar.copy(
+                out=wo_bf[:, 4 * n0 : 4 * n1].rearrange("p (c i t) -> p c t i", t=4, i=4),
+                in_=wo_raw[:, :, n0:n1].rearrange("p t (c i) -> p c t i", i=4),
+            )
+        h_bf = [product_on_gpsimd(0, cell_chunk(0, False))]
+        words[PAGE, 1, 1] = gather_words(PAGE, 1, HALF, HALF, "wr1", 64 - 2048)[:]
+        gather_group("late12", [(PRED, 1, 1), (TOKEN, 0, 2), (TOKEN, 1, 2), (PRED, 0, 2), (PRED, 1, 2)], "wr1", 64)
+        cell1 = cell_chunk(1, False)
+        page_half(1)
+        cell2 = cell_chunk(2, False)
+        wo_q = [quantize("wo_a", wo_bf[:, : 4 * 256], 256), quantize("wo_b", wo_bf[:, 4 * 256 :], 128)]
+        wo_tiles = [(wo_q[0], 0), (wo_q[0], P), (wo_q[1], 0)]
+        gather_group("token3", [(TOKEN, a, 3) for a in range(PASSES)], "wo")
+        project(0, CHUNK, quantize("h0", h_bf[0][:], CHUNK), 4)
+        project(CHUNK, CHUNK, quantize("h1", product_on_vector("h1", gates[1], cell1[:], CHUNK)[:], CHUNK), 6)
+        gather_group("pred3", [(PRED, a, 3) for a in range(PASSES)], "h1", -64)
+        cell3 = cell_chunk(3, True)
+        project(2 * CHUNK, CHUNK, quantize("h2", product_on_vector("h2", gates[2], cell2[:], CHUNK)[:], CHUNK), 4)
+        for u in range(2):
+            last = product_on_vector(
+                "h3_%d" % u, gates[3][:, :, u * UNIT : (u + 1) * UNIT], cell3[:, 512 * u : 512 * (u + 1)], UNIT
+            )
+            project(3 * CHUNK + u * UNIT, UNIT, quantize("h3_%d" % u, last[:], UNIT), 6 + u)

@@ -23,10 +23,9 @@ HALF = 512
 CHUNK = 256
 UNIT = 128
 PAGE, TOKEN, PRED = 0, 1, 2
-SLOTS = {"wp1": 0, "page": 4096, "wr0": 4096 + 2048, "wr1": 14336 + 2048, "wo": 26624, "h0": 26624 + 3072, "h1": 26624 + 3072,
-         "cell0": 32768, "gate1": 32768}
 LOAD = 8192
-LOADS = ("wt_raw", "wp_raw0", "wp_raw1", "tab0", "tab1", "wr_raw0", "wr_raw1", "wo_raw", "gain")
+LOADS = ("wt_raw", "tab0", "tab1", "wp_raw0", "wr_raw1", "wp_raw1", "wr_raw0", "wo_raw")
+CHUNKS = (256, 256, 256, 128, 128)
 
 
 def tile_list_paged_memory_cell_kernel(
@@ -35,7 +34,6 @@ def tile_list_paged_memory_cell_kernel(
     nc = tc.nc
     with ExitStack() as ctx:
         keep = ctx.enter_context(tc.tile_pool(name="keep", bufs=1))
-        shared = ctx.enter_context(tc.tile_pool(name="shared", bufs=1))
         psum = ctx.enter_context(tc.psum_pool(name="psum", bufs=1))
 
         front = ctx.enter_context(tc.tile_pool(name="front", bufs=1))
@@ -43,9 +41,7 @@ def tile_list_paged_memory_cell_kernel(
         def tile(name, shape, dtype, slot=None, at=0):
             if name in LOADS or slot in LOADS:
                 return front.tile(shape, dtype, name=name, offset=LOADS.index(slot or name) * LOAD + at, align_bytes=64)
-            if slot not in SLOTS:
-                return keep.tile(shape, dtype, name=name, align_bytes=64)
-            return shared.tile(shape, dtype, name=name, offset=SLOTS[slot] + at, align_bytes=64)
+            return keep.tile(shape, dtype, name=name, align_bytes=64)
 
         def bank(b):
             return psum.tile([P, 512], F32, name="bank%d" % b)
@@ -93,13 +89,8 @@ def tile_list_paged_memory_cell_kernel(
                 out=wt_sc_raw[32 * q : 32 * q + 4, :].bitcast(I32).rearrange("r (a w) -> r a w", a=PASSES),
                 in_=wt_scales[:, 4 * q : 4 * q + 4, :].bitcast(I32).rearrange("a r w -> r a w"),
             )
-        tab.append(load_table(1))
         wr_raw = [load_rows("wr_raw0", wr, 0)]
-        gain = [tile("gain%d" % t, [P, 1], F32, "gain", 64 * t) for t in range(4)]
-        g_rows = g.rearrange("(c t i o) -> t c i o", t=4, i=4, o=1)
-        with nc.allow_non_contiguous_dma(reason="one gain value for each partition"):
-            for t in range(4):
-                nc.sync.dma_start(out=gain[t][:], in_=g_rows[t])
+        tab.append(load_table(1))
         wr_raw.append(load_rows("wr_raw1", wr, 1))
         wo_raw = tile("wo_raw", [P, 4, N], F32)
         wo_rows = wo.rearrange("(c t i) n -> t c i n", t=4, i=4)
@@ -117,19 +108,18 @@ def tile_list_paged_memory_cell_kernel(
         def gather_words(n, a, s0, count, slot=None, at=0):
             return gather("w%d_%d_%d" % (n, a, s0), tab[a][:].bitcast(U32), n, s0, count, U32, slot, at)
 
-        def round_weight(name, raw, on_scalar):
-            grouped = tile(name + "_bf", [P, 4 * H], BF16, name)
+        def round_on_scalar(grouped, raw, on_scalar):
             dst = grouped[:].rearrange("p (t c i j) -> p t c j i", t=4, i=4, j=4)
             src = raw[:].rearrange("p j (c t i) -> p t c j i", t=4, i=4)
-            if on_scalar:
-                nc.scalar.copy(out=dst[:, :on_scalar], in_=src[:, :on_scalar])
+            nc.scalar.copy(out=dst[:, :on_scalar], in_=src[:, :on_scalar])
+
+        def round_on_gpsimd(grouped, raw, on_scalar):
             for t in range(on_scalar, 4):
                 nc.gpsimd.tensor_scalar(
                     out=grouped[:, H * t : H * (t + 1)].rearrange("p (c i j) -> p c i j", i=4, j=4),
                     in0=raw[:].rearrange("p j (c t i) -> p t c i j", t=4, i=4)[:, t],
                     scalar1=1.0, scalar2=0.0, op0=MULT, op1=ADD,
                 )
-            return grouped
 
         def quantize(name, grouped, width):
             codes = tile(name + "_codes", [P, width], U32)
@@ -160,9 +150,25 @@ def tile_list_paged_memory_cell_kernel(
             in_=wt_sc_raw[:].bitcast(I32).rearrange("p (a c t) -> p a t c", a=PASSES, t=4),
         )
 
+        wp_bf = [tile("wp_bf%d" % a, [P, 4 * H], BF16) for a in range(PASSES)]
+        wr_bf = [tile("wr_bf0", [P, 4 * H], BF16, "wt_raw", 2048), tile("wr_bf1", [P, 4 * H], BF16)]
+        for grouped, raw in ((wp_bf[0], wp_raw[0]), (wp_bf[1], wp_raw[1]), (wr_bf[0], wr_raw[0])):
+            round_on_scalar(grouped, raw, 4)
+        round_on_gpsimd(wr_bf[1], wr_raw[1], 2)
+        tok_sc0 = gather_scales(TOKEN, 0, S)
+        nc.gpsimd.dma_start(out=tok_sc1[0:100, :].bitcast(I32), in_=tok_sc0[4:104, :].bitcast(I32))
+        gain = [tile("gain%d" % t, [P, 1], F32, "wo_raw", 4 * 4 * N + 64 * t) for t in range(4)]
+        g_rows = g.rearrange("(c t i o) -> t c i o", t=4, i=4, o=1)
+        with nc.allow_non_contiguous_dma(reason="one gain value for each partition"):
+            for t in range(4):
+                nc.gpsimd.dma_start(out=gain[t][:], in_=g_rows[t])
+        page_sc = gather_scales(PAGE, 0, S)
+        pred_sc = gather_scales(PRED, 0, S)
+        wp_q = [quantize("wp%d" % a, wp_bf[a][:], H) for a in range(PASSES)]
+
         words = {}
         gates = []
-        wp_bf = [round_weight("wp%d" % a, wp_raw[a], 4) for a in range(PASSES)]
+        cells = []
 
         def page_half(half):
             banks = [bank(4 * half + t) for t in range(4)]
@@ -170,89 +176,96 @@ def tile_list_paged_memory_cell_kernel(
             for a in range(PASSES):
                 for t in range(4):
                     fp8_pass(banks[t][:], t, wp_q[a], words[PAGE, a, half], page_sc[4 * a : P, cols], a == 0, a == 1)
-            sig = tile("sig%d" % half, [P, 4, HALF], F32, "wr_raw%d" % half)
-            gate = tile("gate%d" % half, [P, 4, HALF], F32, "gate%d" % half)
+            sig = tile("sig%d" % half, [P, 4, HALF], F32, ("wp_raw1", "wp_raw0")[half], 64)
+            gate = tile("gate%d" % half, [P, 4, HALF], F32)
             for t in range(4):
                 nc.scalar.activation(out=sig[:, t, :], in_=banks[t][:], func=ACT.Sigmoid)
             for t in range(4):
                 nc.gpsimd.tensor_scalar(
                     out=gate[:, t, :], in0=sig[:, t, :], scalar1=gain[t][:], scalar2=0.0, op0=MULT, op1=ADD
                 )
-            gates.extend([gate[:, :, :CHUNK], gate[:, :, CHUNK:]])
+            gates.append(gate)
 
-        def gather_group(name, keys, slot, at=0):
-            group = tile(name, [P, len(keys) * CHUNK], U32, slot, at)
-            for place, (n, a, q) in enumerate(keys):
-                dst = group[:, place * CHUNK : (place + 1) * CHUNK]
-                cols = slice(q * CHUNK // 16, (q + 1) * CHUNK // 16)
-                nc.vector.tensor_copy(dst, tab[a][:].bitcast(U32).indirect(lists[n][:, cols]))
-                words[n, a, q] = dst
-
-        def cell_chunk(q, by_unit):
-            banks = [bank(2 * (q % 2) + j) for j in range(2)]
-            passes = []
-            for a in range(PASSES):
-                for u in range(2):
-                    for t in range(4):
-                        passes.append((TOKEN, a, t, u * UNIT, UNIT))
-            for a in range(PASSES):
-                for u in range(2 if by_unit else 1):
-                    for t in range(4):
-                        passes.append((PRED, a, t, u * UNIT, UNIT if by_unit else CHUNK))
-            places = [(s0 // UNIT, t * UNIT) if by_unit else (t // 2, (t % 2) * CHUNK + s0) for n, a, t, s0, w in passes]
-            which = [b for b, c in places]
-            for k, (n, a, t, s0, width) in enumerate(passes):
-                b, col = places[k]
-                start = b not in which[:k]
-                stop = b not in which[k + 1 :]
-                dst = banks[b][:, col : col + width]
-                moving = words[n, a, q][:, s0 : s0 + width]
-                j0 = q * CHUNK + s0
-                if n == PRED:
-                    scales = pred_sc[j0 // HALF][4 * a : P, j0 % HALF : j0 % HALF + width]
-                    fp8_pass(dst, t, wr_q[a], moving, scales, start, stop)
-                else:
+        def cell_half(half):
+            banks = [bank(4 * half + t) for t in range(4)]
+            cols = slice(half * HALF, (half + 1) * HALF)
+            for n, a in ((TOKEN, 0), (PRED, 0), (TOKEN, 1), (PRED, 1)):
+                for t in range(4):
+                    if n == PRED:
+                        fp8_pass(banks[t][:], t, wr_q[a], words[n, a, half], pred_sc[4 * a : P, cols], False, a == 1)
+                        continue
                     w0 = (4 * a + t) * (P // 2)
                     c0 = (4 * a + t) * (P // 4)
                     nc.tensor.matmul_mx(
-                        out=dst,
+                        out=banks[t][:],
                         lhsT=wt_codes[:, w0 : w0 + P // 2].bitcast(FP4X4),
                         lhsT_scale=wt_sc[:, c0 : c0 + P // 4].bitcast(U8),
-                        rhs=moving.bitcast(FP8X4),
-                        rhs_scale=(tok_sc0, tok_sc1)[a][:, j0 : j0 + width],
-                        start=start,
-                        stop=stop,
+                        rhs=words[n, a, half].bitcast(FP8X4),
+                        rhs_scale=(tok_sc0, tok_sc1)[a][:, cols],
+                        start=a == 0,
+                        stop=False,
                     )
-            cell = tile("cell%d" % q, [P, 2 * 512], F32, "cell%d" % q)
-            for b in range(2):
-                nc.scalar.activation(out=cell[:, 512 * b : 512 * (b + 1)], in_=banks[b][:], func=ACT.Tanh)
-            return cell
+            width = CHUNK if half else HALF
+            for s0 in range(0, HALF, width):
+                cell = tile("cell%d_%d" % (half, s0), [P, 4, width], F32)
+                for t in range(4):
+                    nc.scalar.activation(out=cell[:, t, :], in_=banks[t][:, s0 : s0 + width], func=ACT.Tanh)
+                cells.extend(cell[:, :, c0 : c0 + CHUNK] for c0 in range(0, width, CHUNK))
 
-        def product_on_gpsimd(q, cells):
-            h_bf = tile("h%d_bf" % q, [P, 4 * CHUNK], BF16, "h%d" % q)
-            for s0 in range(0, CHUNK, UNIT):
-                nc.gpsimd.tensor_tensor(
-                    out=h_bf[:, 4 * s0 : 4 * (s0 + UNIT)].rearrange("p (s t) -> p s t", t=4),
-                    in0=gates[q][:, :, s0 : s0 + UNIT].rearrange("p t s -> p s t"),
-                    in1=cells[:].rearrange("p (t s) -> p s t", t=4)[:, s0 : s0 + UNIT],
-                    op=MULT,
-                )
-            return h_bf
+        def pick(n, a, half, slot=None, at=0):
+            words[n, a, half] = gather_words(n, a, half * HALF, HALF, slot, at)[:]
 
+        pick(PAGE, 0, 0)
+        pick(PAGE, 0, 1)
+        pick(PRED, 0, 0)
+        pick(PAGE, 1, 0)
+        wr_q = [quantize("wr0", wr_bf[0][:], H)]
+        page_half(0)
+        pick(PAGE, 1, 1)
+        round_on_scalar(wr_bf[1], wr_raw[1], 2)
+        page_half(1)
+        pick(TOKEN, 0, 0, "wt_raw", 2048)
+        pick(TOKEN, 1, 0)
+        pick(PRED, 1, 0)
+        wr_q.append(quantize("wr1", wr_bf[1][:], H))
+        wo_bf = tile("wo_bf", [P, 4 * N], BF16, "wp_raw1", 64)
+        nc.scalar.copy(
+            out=wo_bf[:].rearrange("p (c i t) -> p c t i", t=4, i=4),
+            in_=wo_raw[:].rearrange("p t (c i) -> p c t i", i=4),
+        )
+        cell_half(0)
+        for place, (n, a) in enumerate(((TOKEN, 0), (PRED, 0), (TOKEN, 1), (PRED, 1))):
+            pick(n, a, 1, "wr_raw1", 64 + 2048 * place)
+        cell_half(1)
+        wo_q = [quantize("wo_a", wo_bf[:, : 4 * 256], 256), quantize("wo_b", wo_bf[:, 4 * 256 :], 128)]
+        wo_tiles = [(wo_q[0], 0), (wo_q[0], P), (wo_q[1], 0)]
         out_rows = out.rearrange("(nt p) s -> p nt s", p=P)
 
-        def project(s0, width, h_q, first_bank):
+        def product(s0, width):
+            h_bf = tile("h_bf%d" % s0, [P, 4 * width], BF16)
+            gate = gates[s0 // HALF][:, :, s0 % HALF : s0 % HALF + width]
+            cell = cells[s0 // CHUNK][:, :, s0 % CHUNK : s0 % CHUNK + width]
+            nc.vector.tensor_tensor(
+                out=h_bf[:].rearrange("p (c i t) -> p c t i", t=4, i=4),
+                in0=gate.rearrange("p t (c i) -> p c t i", i=4),
+                in1=cell.rearrange("p t (c i) -> p c t i", i=4),
+                op=MULT,
+            )
+            return h_bf
+
+        def project(s0, width, h_bf):
+            h_codes, h_scales = quantize("h%d" % s0, h_bf[:], width)
             state = tile("state%d" % s0, [P, 3, width], F32)
             for u0 in range(0, width, UNIT):
-                dst = bank(first_bank + u0 // UNIT)
+                dst = bank((s0 + u0) // UNIT)
                 for nt in range(3):
                     (codes, scales), m0 = wo_tiles[nt]
                     nc.tensor.matmul_mx(
                         out=dst[:, nt * UNIT : (nt + 1) * UNIT],
                         lhsT=codes[:, m0 : m0 + P].bitcast(FP8X4),
                         lhsT_scale=scales[:, m0 : m0 + P],
-                        rhs=h_q[0][:, u0 : u0 + UNIT].bitcast(FP8X4),
-                        rhs_scale=h_q[1][:, u0 : u0 + UNIT],
+                        rhs=h_codes[:, u0 : u0 + UNIT].bitcast(FP8X4),
+                        rhs_scale=h_scales[:, u0 : u0 + UNIT],
                         start=True,
                         stop=True,
                     )
@@ -263,54 +276,9 @@ def tile_list_paged_memory_cell_kernel(
                 )
             nc.sync.dma_start(out=out_rows[:, :, s0 : s0 + width], in_=state[:])
 
-        def product_on_vector(name, gate, cell, width):
-            h_bf = tile(name + "_bf", [P, 4 * width], BF16, name)
-            nc.vector.tensor_tensor(
-                out=h_bf[:].rearrange("p (c i t) -> p c t i", t=4, i=4),
-                in0=gate.rearrange("p t (c i) -> p c t i", i=4),
-                in1=cell.rearrange("p (t c i) -> p c t i", t=4, i=4),
-                op=MULT,
-            )
-            return h_bf
-
-        tok_sc0 = gather_scales(TOKEN, 0, S)
-        nc.gpsimd.dma_start(out=tok_sc1[0:100, :].bitcast(I32), in_=tok_sc0[4:104, :].bitcast(I32))
-        page_sc = gather_scales(PAGE, 0, S)
-        pred_all = gather_scales(PRED, 0, S)
-        pred_sc = [pred_all[:, :HALF], pred_all[:, HALF:]]
-        wp_q = [quantize("wp%d" % a, wp_bf[a][:], H) for a in range(PASSES)]
-        wr_bf = [round_weight("wr0", wr_raw[0], 3), round_weight("wr1", wr_raw[1], 2)]
-        words[PAGE, 0, 0] = gather_words(PAGE, 0, 0, HALF)[:]
-        gather_group("chunk0_a", [(TOKEN, 0, 0), (PRED, 0, 0), (TOKEN, 0, 1)], "wp1")
-        words[PAGE, 1, 0] = gather_words(PAGE, 1, 0, HALF)[:]
-        page_half(0)
-        gather_group("chunk0_b", [(TOKEN, 1, 0), (PRED, 1, 0)], "none")
-        wr_q = [quantize("wr0", wr_bf[0][:], H)]
-        words[PAGE, 0, 1] = gather_words(PAGE, 0, HALF, HALF, "wr0", 0)[:]
-        gather_group("early1", [(TOKEN, 1, 1), (PRED, 0, 1)], "wr0", 2048)
-        wr_q.append(quantize("wr1", wr_bf[1][:], H))
-        wo_bf = tile("wo_bf", [P, 4 * N], BF16, "wo")
-        for n0, n1 in ((0, 256), (256, N)):
-            nc.scalar.copy(
-                out=wo_bf[:, 4 * n0 : 4 * n1].rearrange("p (c i t) -> p c t i", t=4, i=4),
-                in_=wo_raw[:, :, n0:n1].rearrange("p t (c i) -> p c t i", i=4),
-            )
-        h_bf = [product_on_gpsimd(0, cell_chunk(0, False))]
-        words[PAGE, 1, 1] = gather_words(PAGE, 1, HALF, HALF, "wr1", 64 - 2048)[:]
-        gather_group("late12", [(PRED, 1, 1), (TOKEN, 0, 2), (TOKEN, 1, 2), (PRED, 0, 2), (PRED, 1, 2)], "wr1", 64)
-        cell1 = cell_chunk(1, False)
-        page_half(1)
-        cell2 = cell_chunk(2, False)
-        wo_q = [quantize("wo_a", wo_bf[:, : 4 * 256], 256), quantize("wo_b", wo_bf[:, 4 * 256 :], 128)]
-        wo_tiles = [(wo_q[0], 0), (wo_q[0], P), (wo_q[1], 0)]
-        gather_group("token3", [(TOKEN, a, 3) for a in range(PASSES)], "wo")
-        project(0, CHUNK, quantize("h0", h_bf[0][:], CHUNK), 4)
-        project(CHUNK, CHUNK, quantize("h1", product_on_vector("h1", gates[1], cell1[:], CHUNK)[:], CHUNK), 6)
-        gather_group("pred3", [(PRED, a, 3) for a in range(PASSES)], "h1", -64)
-        cell3 = cell_chunk(3, True)
-        project(2 * CHUNK, CHUNK, quantize("h2", product_on_vector("h2", gates[2], cell2[:], CHUNK)[:], CHUNK), 4)
-        for u in range(2):
-            last = product_on_vector(
-                "h3_%d" % u, gates[3][:, :, u * UNIT : (u + 1) * UNIT], cell3[:, 512 * u : 512 * (u + 1)], UNIT
-            )
-            project(3 * CHUNK + u * UNIT, UNIT, quantize("h3_%d" % u, last[:], UNIT), 6 + u)
+        starts = [sum(CHUNKS[:k]) for k in range(len(CHUNKS))]
+        made = [product(starts[0], CHUNKS[0])]
+        for k in range(len(CHUNKS)):
+            if k + 1 < len(CHUNKS):
+                made.append(product(starts[k + 1], CHUNKS[k + 1]))
+            project(starts[k], CHUNKS[k], made[k])

@@ -24,8 +24,8 @@ CHUNK = 256
 UNIT = 128
 PAGE, TOKEN, PRED = 0, 1, 2
 LOAD = 8192
-LOADS = ("wt_raw", "tab0", "tab1", "wp_raw0", "wr_raw1", "wp_raw1", "wr_raw0", "wo_raw")
-CHUNKS = (256, 256, 256, 128, 128)
+LOADS = ("wt_raw", "tab0", "tab1", "wp_raw0", "wr_raw1", "wp_raw1", "wr_raw0", "wo_raw", "spare")
+STORES = (256, 256, 256, 128, 128)
 
 
 def tile_list_paged_memory_cell_kernel(
@@ -82,13 +82,13 @@ def tile_list_paged_memory_cell_kernel(
         wp_raw = [load_rows("wp_raw0", wp, 0)]
         wt_raw = tile("wt_raw", [P, PASSES, H // 2], I32)
         nc.sync.dma_start(out=wt_raw[:], in_=wt_words.bitcast(I32).rearrange("a p w -> p a w"))
-        wp_raw.append(load_rows("wp_raw1", wp, 1))
-        tab = [load_table(0)]
         for q in range(4):
             nc.sync.dma_start(
                 out=wt_sc_raw[32 * q : 32 * q + 4, :].bitcast(I32).rearrange("r (a w) -> r a w", a=PASSES),
                 in_=wt_scales[:, 4 * q : 4 * q + 4, :].bitcast(I32).rearrange("a r w -> r a w"),
             )
+        wp_raw.append(load_rows("wp_raw1", wp, 1))
+        tab = [load_table(0)]
         wr_raw = [load_rows("wr_raw0", wr, 0)]
         tab.append(load_table(1))
         wr_raw.append(load_rows("wr_raw1", wr, 1))
@@ -151,10 +151,9 @@ def tile_list_paged_memory_cell_kernel(
         )
 
         wp_bf = [tile("wp_bf%d" % a, [P, 4 * H], BF16) for a in range(PASSES)]
-        wr_bf = [tile("wr_bf0", [P, 4 * H], BF16, "wt_raw", 2048), tile("wr_bf1", [P, 4 * H], BF16)]
+        wr_bf = [tile("wr_bf0", [P, 4 * H], BF16, "wt_raw", 2048), tile("wr_bf1", [P, 4 * H], BF16, "spare")]
         for grouped, raw in ((wp_bf[0], wp_raw[0]), (wp_bf[1], wp_raw[1]), (wr_bf[0], wr_raw[0])):
             round_on_scalar(grouped, raw, 4)
-        round_on_gpsimd(wr_bf[1], wr_raw[1], 2)
         tok_sc0 = gather_scales(TOKEN, 0, S)
         nc.gpsimd.dma_start(out=tok_sc1[0:100, :].bitcast(I32), in_=tok_sc0[4:104, :].bitcast(I32))
         gain = [tile("gain%d" % t, [P, 1], F32, "wo_raw", 4 * 4 * N + 64 * t) for t in range(4)]
@@ -176,8 +175,8 @@ def tile_list_paged_memory_cell_kernel(
             for a in range(PASSES):
                 for t in range(4):
                     fp8_pass(banks[t][:], t, wp_q[a], words[PAGE, a, half], page_sc[4 * a : P, cols], a == 0, a == 1)
-            sig = tile("sig%d" % half, [P, 4, HALF], F32, ("wp_raw1", "wp_raw0")[half], 64)
-            gate = tile("gate%d" % half, [P, 4, HALF], F32)
+            sig = tile("sig%d" % half, [P, 4, HALF], F32, ("wp_raw1", "wp_raw0")[half], (64, 0)[half])
+            gate = tile("gate%d" % half, [P, 4, HALF], F32, "spare" if half else None)
             for t in range(4):
                 nc.scalar.activation(out=sig[:, t, :], in_=banks[t][:], func=ACT.Sigmoid)
             for t in range(4):
@@ -205,12 +204,13 @@ def tile_list_paged_memory_cell_kernel(
                         start=a == 0,
                         stop=False,
                     )
-            width = CHUNK if half else HALF
-            for s0 in range(0, HALF, width):
-                cell = tile("cell%d_%d" % (half, s0), [P, 4, width], F32)
-                for t in range(4):
-                    nc.scalar.activation(out=cell[:, t, :], in_=banks[t][:, s0 : s0 + width], func=ACT.Tanh)
-                cells.extend(cell[:, :, c0 : c0 + CHUNK] for c0 in range(0, width, CHUNK))
+            return banks
+
+        def squash(banks, s0, width):
+            cell = tile("cell%d" % len(cells), [P, 4, width], F32)
+            for t in range(4):
+                nc.scalar.activation(out=cell[:, t, :], in_=banks[t][:, s0 : s0 + width], func=ACT.Tanh)
+            cells.extend(cell[:, :, c0 : c0 + CHUNK] for c0 in range(0, width, CHUNK))
 
         def pick(n, a, half, slot=None, at=0):
             words[n, a, half] = gather_words(n, a, half * HALF, HALF, slot, at)[:]
@@ -222,23 +222,24 @@ def tile_list_paged_memory_cell_kernel(
         wr_q = [quantize("wr0", wr_bf[0][:], H)]
         page_half(0)
         pick(PAGE, 1, 1)
-        round_on_scalar(wr_bf[1], wr_raw[1], 2)
+        round_on_scalar(wr_bf[1], wr_raw[1], 3)
+        round_on_gpsimd(wr_bf[1], wr_raw[1], 3)
         page_half(1)
         pick(TOKEN, 0, 0, "wt_raw", 2048)
         pick(TOKEN, 1, 0)
         pick(PRED, 1, 0)
+        pick(TOKEN, 0, 1, "wt_raw", 4096)
         wr_q.append(quantize("wr1", wr_bf[1][:], H))
         wo_bf = tile("wo_bf", [P, 4 * N], BF16, "wp_raw1", 64)
         nc.scalar.copy(
             out=wo_bf[:].rearrange("p (c i t) -> p c t i", t=4, i=4),
             in_=wo_raw[:].rearrange("p t (c i) -> p c t i", i=4),
         )
-        cell_half(0)
-        for place, (n, a) in enumerate(((TOKEN, 0), (PRED, 0), (TOKEN, 1), (PRED, 1))):
-            pick(n, a, 1, "wr_raw1", 64 + 2048 * place)
-        cell_half(1)
-        wo_q = [quantize("wo_a", wo_bf[:, : 4 * 256], 256), quantize("wo_b", wo_bf[:, 4 * 256 :], 128)]
-        wo_tiles = [(wo_q[0], 0), (wo_q[0], P), (wo_q[1], 0)]
+        squash(cell_half(0), 0, HALF)
+        for place, (n, a) in enumerate(((PRED, 0), (TOKEN, 1), (PRED, 1))):
+            pick(n, a, 1, "wr_raw1", 2048 * place)
+        last_banks = cell_half(1)
+        squash(last_banks, 0, CHUNK)
         out_rows = out.rearrange("(nt p) s -> p nt s", p=P)
 
         def product(s0, width):
@@ -253,32 +254,36 @@ def tile_list_paged_memory_cell_kernel(
             )
             return h_bf
 
-        def project(s0, width, h_bf):
-            h_codes, h_scales = quantize("h%d" % s0, h_bf[:], width)
+        def project(s0, h_bf, state):
+            h_codes, h_scales = quantize("h%d" % s0, h_bf[:], UNIT)
+            dst = bank(s0 // UNIT)
+            for nt in range(3):
+                (codes, scales), m0 = wo_tiles[nt]
+                nc.tensor.matmul_mx(
+                    out=dst[:, nt * UNIT : (nt + 1) * UNIT],
+                    lhsT=codes[:, m0 : m0 + P].bitcast(FP8X4),
+                    lhsT_scale=scales[:, m0 : m0 + P],
+                    rhs=h_codes[:].bitcast(FP8X4),
+                    rhs_scale=h_scales[:],
+                    start=True,
+                    stop=True,
+                )
+            nc.scalar.activation(
+                out=state, in_=dst[:, : 3 * UNIT].rearrange("p (nt s) -> p nt s", nt=3), func=ACT.Tanh
+            )
+
+        made = [product(0, UNIT)]
+        wo_q = [quantize("wo_a", wo_bf[:, : 4 * 256], 256), quantize("wo_b", wo_bf[:, 4 * 256 :], 128)]
+        wo_tiles = [(wo_q[0], 0), (wo_q[0], P), (wo_q[1], 0)]
+        s0 = 0
+        for width in STORES:
             state = tile("state%d" % s0, [P, 3, width], F32)
             for u0 in range(0, width, UNIT):
-                dst = bank((s0 + u0) // UNIT)
-                for nt in range(3):
-                    (codes, scales), m0 = wo_tiles[nt]
-                    nc.tensor.matmul_mx(
-                        out=dst[:, nt * UNIT : (nt + 1) * UNIT],
-                        lhsT=codes[:, m0 : m0 + P].bitcast(FP8X4),
-                        lhsT_scale=scales[:, m0 : m0 + P],
-                        rhs=h_codes[:, u0 : u0 + UNIT].bitcast(FP8X4),
-                        rhs_scale=h_scales[:, u0 : u0 + UNIT],
-                        start=True,
-                        stop=True,
-                    )
-                nc.scalar.activation(
-                    out=state[:, :, u0 : u0 + UNIT],
-                    in_=dst[:, : 3 * UNIT].rearrange("p (nt s) -> p nt s", nt=3),
-                    func=ACT.Tanh,
-                )
-            nc.sync.dma_start(out=out_rows[:, :, s0 : s0 + width], in_=state[:])
-
-        starts = [sum(CHUNKS[:k]) for k in range(len(CHUNKS))]
-        made = [product(starts[0], CHUNKS[0])]
-        for k in range(len(CHUNKS)):
-            if k + 1 < len(CHUNKS):
-                made.append(product(starts[k + 1], CHUNKS[k + 1]))
-            project(starts[k], CHUNKS[k], made[k])
+                if s0 + u0 + UNIT < S:
+                    made.append(product(s0 + u0 + UNIT, UNIT))
+                project(s0 + u0, made[(s0 + u0) // UNIT], state[:, :, u0 : u0 + UNIT])
+            queue = nc.scalar if s0 + width == S else nc.sync
+            queue.dma_start(out=out_rows[:, :, s0 : s0 + width], in_=state[:])
+            if s0 == 0:
+                squash(last_banks, CHUNK, CHUNK)
+            s0 = s0 + width

@@ -80,6 +80,10 @@ def tile_list_paged_memory_cell_kernel(
                 in_=tab_scales[:, 4 * q : 4 * q + 4, :].bitcast(I32),
             )
         wp_raw = [load_rows("wp_raw0", wp, 0)]
+        wp_raw.append(load_rows("wp_raw1", wp, 1))
+        tab = [load_table(0)]
+        wr_raw = [load_rows("wr_raw0", wr, 0)]
+        tab.append(load_table(1))
         wt_raw = tile("wt_raw", [P, PASSES, H // 2], I32)
         nc.sync.dma_start(out=wt_raw[:], in_=wt_words.bitcast(I32).rearrange("a p w -> p a w"))
         for q in range(4):
@@ -87,10 +91,6 @@ def tile_list_paged_memory_cell_kernel(
                 out=wt_sc_raw[32 * q : 32 * q + 4, :].bitcast(I32).rearrange("r (a w) -> r a w", a=PASSES),
                 in_=wt_scales[:, 4 * q : 4 * q + 4, :].bitcast(I32).rearrange("a r w -> r a w"),
             )
-        wp_raw.append(load_rows("wp_raw1", wp, 1))
-        tab = [load_table(0)]
-        wr_raw = [load_rows("wr_raw0", wr, 0)]
-        tab.append(load_table(1))
         wr_raw.append(load_rows("wr_raw1", wr, 1))
         wo_raw = tile("wo_raw", [P, 4, N], F32)
         wo_rows = wo.rearrange("(c t i) n -> t c i n", t=4, i=4)
@@ -175,7 +175,7 @@ def tile_list_paged_memory_cell_kernel(
             for a in range(PASSES):
                 for t in range(4):
                     fp8_pass(banks[t][:], t, wp_q[a], words[PAGE, a, half], page_sc[4 * a : P, cols], a == 0, a == 1)
-            sig = tile("sig%d" % half, [P, 4, HALF], F32, ("wp_raw1", "wp_raw0")[half], (64, 0)[half])
+            sig = tile("sig%d" % half, [P, 4, HALF], F32, ("wp_raw1", "wp_raw0")[half], 64)
             gate = tile("gate%d" % half, [P, 4, HALF], F32, "spare" if half else None)
             for t in range(4):
                 nc.scalar.activation(out=sig[:, t, :], in_=banks[t][:], func=ACT.Sigmoid)
@@ -218,26 +218,28 @@ def tile_list_paged_memory_cell_kernel(
         pick(PAGE, 0, 0)
         pick(PAGE, 0, 1)
         pick(PRED, 0, 0)
-        pick(PAGE, 1, 0)
         wr_q = [quantize("wr0", wr_bf[0][:], H)]
-        page_half(0)
-        pick(PAGE, 1, 1)
-        round_on_scalar(wr_bf[1], wr_raw[1], 3)
+        pick(PAGE, 1, 0, "wr_raw0", 2048)
         round_on_gpsimd(wr_bf[1], wr_raw[1], 3)
+        page_half(0)
+        pick(PAGE, 1, 1, "wr_raw0", 4096)
+        round_on_scalar(wr_bf[1], wr_raw[1], 3)
         page_half(1)
-        pick(TOKEN, 0, 0, "wt_raw", 2048)
-        pick(TOKEN, 1, 0)
-        pick(PRED, 1, 0)
-        pick(TOKEN, 0, 1, "wt_raw", 4096)
+        pick(TOKEN, 0, 0, "wt_raw", 2048 + 64)
+        pick(TOKEN, 1, 0, "wr_raw0", 6144)
+        pick(PRED, 1, 0, "wt_raw", 64)
+        pick(TOKEN, 0, 1, "wt_raw", 4096 + 64)
         wr_q.append(quantize("wr1", wr_bf[1][:], H))
         wo_bf = tile("wo_bf", [P, 4 * N], BF16, "wp_raw1", 64)
         nc.scalar.copy(
             out=wo_bf[:].rearrange("p (c i t) -> p c t i", t=4, i=4),
             in_=wo_raw[:].rearrange("p t (c i) -> p c t i", i=4),
         )
-        squash(cell_half(0), 0, HALF)
+        first_banks = cell_half(0)
+        for s0 in range(0, HALF, CHUNK):
+            squash(first_banks, s0, CHUNK)
         for place, (n, a) in enumerate(((PRED, 0), (TOKEN, 1), (PRED, 1))):
-            pick(n, a, 1, "wr_raw1", 2048 * place)
+            pick(n, a, 1, "wr_raw1", 2048 * (place + 1))
         last_banks = cell_half(1)
         squash(last_banks, 0, CHUNK)
         out_rows = out.rearrange("(nt p) s -> p nt s", p=P)

@@ -25,7 +25,7 @@ UNIT = 128
 PAGE, TOKEN, PRED = 0, 1, 2
 LOAD = 8192
 LOADS = ("wt_raw", "tab0", "tab1", "wp_raw0", "wr_raw1", "wp_raw1", "wr_raw0", "wo_raw", "spare")
-STORES = (256, 256, 256, 128, 128)
+STORES = ((128, 128), (128, 128), (128, 128), (128,), (128,))
 
 
 def tile_list_paged_memory_cell_kernel(
@@ -52,8 +52,8 @@ def tile_list_paged_memory_cell_kernel(
         wt_sc_raw = tile("wt_sc_raw", [P, PASSES * H], U8)
         tok_sc1 = tile("tok_sc1", [P, S], U8)
         warm = tile("warm", [P, 2], F32)
-        nc.vector.memset(warm[:, 0:1], 0.0)
         nc.vector.memset(zeros[:, : PASSES * H // 4], 0)
+        nc.gpsimd.memset(warm[:, 0:1], 0.0)
         nc.vector.tensor_copy(out=wt_sc_raw[:].bitcast(I32), in_=zeros[:, : PASSES * H // 4])
         nc.gpsimd.memset(tok_sc1[:].bitcast(I32), 0)
         nc.scalar.activation(out=warm[:, 1:2], in_=warm[:, 0:1], func=ACT.Sigmoid)
@@ -81,21 +81,21 @@ def tile_list_paged_memory_cell_kernel(
             )
         wp_raw = [load_rows("wp_raw0", wp, 0)]
         wp_raw.append(load_rows("wp_raw1", wp, 1))
-        tab = [load_table(0)]
-        wr_raw = [load_rows("wr_raw0", wr, 0)]
-        tab.append(load_table(1))
-        wt_raw = tile("wt_raw", [P, PASSES, H // 2], I32)
-        nc.sync.dma_start(out=wt_raw[:], in_=wt_words.bitcast(I32).rearrange("a p w -> p a w"))
         for q in range(4):
             nc.sync.dma_start(
                 out=wt_sc_raw[32 * q : 32 * q + 4, :].bitcast(I32).rearrange("r (a w) -> r a w", a=PASSES),
                 in_=wt_scales[:, 4 * q : 4 * q + 4, :].bitcast(I32).rearrange("a r w -> r a w"),
             )
-        wr_raw.append(load_rows("wr_raw1", wr, 1))
+        tab = [load_table(0)]
+        wr_raw = [load_rows("wr_raw0", wr, 0)]
+        tab.append(load_table(1))
+        wt_raw = tile("wt_raw", [P, PASSES, H // 2], I32)
+        nc.sync.dma_start(out=wt_raw[:], in_=wt_words.bitcast(I32).rearrange("a p w -> p a w"))
         wo_raw = tile("wo_raw", [P, 4, N], F32)
         wo_rows = wo.rearrange("(c t i) n -> t c i n", t=4, i=4)
         for t in range(4):
             nc.sync.dma_start(out=wo_raw[:, t, :], in_=wo_rows[t])
+        wr_raw.append(load_rows("wr_raw1", wr, 1))
 
         def gather(name, window, n, s0, count, dtype, slot=None, at=0):
             picked = tile(name, [P, count], dtype, slot, at)
@@ -113,16 +113,8 @@ def tile_list_paged_memory_cell_kernel(
             src = raw[:].rearrange("p j (c t i) -> p t c j i", t=4, i=4)
             nc.scalar.copy(out=dst[:, :on_scalar], in_=src[:, :on_scalar])
 
-        def round_on_gpsimd(grouped, raw, on_scalar):
-            for t in range(on_scalar, 4):
-                nc.gpsimd.tensor_scalar(
-                    out=grouped[:, H * t : H * (t + 1)].rearrange("p (c i j) -> p c i j", i=4, j=4),
-                    in0=raw[:].rearrange("p j (c t i) -> p t c i j", t=4, i=4)[:, t],
-                    scalar1=1.0, scalar2=0.0, op0=MULT, op1=ADD,
-                )
-
-        def quantize(name, grouped, width):
-            codes = tile(name + "_codes", [P, width], U32)
+        def quantize(name, grouped, width, slot=None, at=0):
+            codes = tile(name + "_codes", [P, width], U32, slot, at)
             scales = tile(name + "_scales", [P, width], U8)
             nc.vector.quantize_mx(out=codes[:].bitcast(FP8X4), scales=scales[:], in_=grouped)
             return codes, scales
@@ -156,11 +148,10 @@ def tile_list_paged_memory_cell_kernel(
             round_on_scalar(grouped, raw, 4)
         tok_sc0 = gather_scales(TOKEN, 0, S)
         nc.gpsimd.dma_start(out=tok_sc1[0:100, :].bitcast(I32), in_=tok_sc0[4:104, :].bitcast(I32))
-        gain = [tile("gain%d" % t, [P, 1], F32, "wo_raw", 4 * 4 * N + 64 * t) for t in range(4)]
-        g_rows = g.rearrange("(c t i o) -> t c i o", t=4, i=4, o=1)
-        with nc.allow_non_contiguous_dma(reason="one gain value for each partition"):
-            for t in range(4):
-                nc.gpsimd.dma_start(out=gain[t][:], in_=g_rows[t])
+        gain = tile("gain", [P, 13], F32, "wo_raw", 4 * 4 * N)
+        g_rows = g.rearrange("(c x) -> c x", x=16)
+        for i in range(4):
+            nc.gpsimd.dma_start(out=gain[i:P:4, :], in_=g_rows[:, i : i + 13])
         page_sc = gather_scales(PAGE, 0, S)
         pred_sc = gather_scales(PRED, 0, S)
         wp_q = [quantize("wp%d" % a, wp_bf[a][:], H) for a in range(PASSES)]
@@ -181,7 +172,7 @@ def tile_list_paged_memory_cell_kernel(
                 nc.scalar.activation(out=sig[:, t, :], in_=banks[t][:], func=ACT.Sigmoid)
             for t in range(4):
                 nc.gpsimd.tensor_scalar(
-                    out=gate[:, t, :], in0=sig[:, t, :], scalar1=gain[t][:], scalar2=0.0, op0=MULT, op1=ADD
+                    out=gate[:, t, :], in0=sig[:, t, :], scalar1=gain[:, 4 * t : 4 * t + 1], scalar2=0.0, op0=MULT, op1=ADD
                 )
             gates.append(gate)
 
@@ -220,21 +211,21 @@ def tile_list_paged_memory_cell_kernel(
         pick(PRED, 0, 0)
         wr_q = [quantize("wr0", wr_bf[0][:], H)]
         pick(PAGE, 1, 0, "wr_raw0", 2048)
-        round_on_gpsimd(wr_bf[1], wr_raw[1], 3)
+        wo_bf = tile("wo_bf", [P, 4 * N], BF16)
+        nc.gpsimd.tensor_scalar(
+            out=wo_bf[:].rearrange("p (n t) -> p n t", t=4),
+            in0=wo_raw[:].rearrange("p t n -> p n t"),
+            scalar1=1.0, scalar2=0.0, op0=MULT, op1=ADD,
+        )
         page_half(0)
         pick(PAGE, 1, 1, "wr_raw0", 4096)
-        round_on_scalar(wr_bf[1], wr_raw[1], 3)
+        round_on_scalar(wr_bf[1], wr_raw[1], 4)
         page_half(1)
         pick(TOKEN, 0, 0, "wt_raw", 2048 + 64)
         pick(TOKEN, 1, 0, "wr_raw0", 6144)
         pick(PRED, 1, 0, "wt_raw", 64)
         pick(TOKEN, 0, 1, "wt_raw", 4096 + 64)
         wr_q.append(quantize("wr1", wr_bf[1][:], H))
-        wo_bf = tile("wo_bf", [P, 4 * N], BF16, "wp_raw1", 64)
-        nc.scalar.copy(
-            out=wo_bf[:].rearrange("p (c i t) -> p c t i", t=4, i=4),
-            in_=wo_raw[:].rearrange("p t (c i) -> p c t i", i=4),
-        )
         first_banks = cell_half(0)
         for s0 in range(0, HALF, CHUNK):
             squash(first_banks, s0, CHUNK)
@@ -256,13 +247,13 @@ def tile_list_paged_memory_cell_kernel(
             )
             return h_bf
 
-        def project(s0, h_bf, state):
-            h_codes, h_scales = quantize("h%d" % s0, h_bf[:], UNIT)
-            dst = bank(s0 // UNIT)
+        def project(k, s0, width, h_bf, state):
+            h_codes, h_scales = quantize("h%d" % s0, h_bf[:], width)
+            dst = bank(k % 8)
             for nt in range(3):
                 (codes, scales), m0 = wo_tiles[nt]
                 nc.tensor.matmul_mx(
-                    out=dst[:, nt * UNIT : (nt + 1) * UNIT],
+                    out=dst[:, nt * width : (nt + 1) * width],
                     lhsT=codes[:, m0 : m0 + P].bitcast(FP8X4),
                     lhsT_scale=scales[:, m0 : m0 + P],
                     rhs=h_codes[:].bitcast(FP8X4),
@@ -271,21 +262,28 @@ def tile_list_paged_memory_cell_kernel(
                     stop=True,
                 )
             nc.scalar.activation(
-                out=state, in_=dst[:, : 3 * UNIT].rearrange("p (nt s) -> p nt s", nt=3), func=ACT.Tanh
+                out=state, in_=dst[:, : 3 * width].rearrange("p (nt s) -> p nt s", nt=3), func=ACT.Tanh
             )
 
-        made = [product(0, UNIT)]
-        wo_q = [quantize("wo_a", wo_bf[:, : 4 * 256], 256), quantize("wo_b", wo_bf[:, 4 * 256 :], 128)]
+        widths = [width for store in STORES for width in store]
+        starts = [sum(widths[:k]) for k in range(len(widths))]
+        made = [product(0, widths[0])]
+        wo_q = [
+            quantize("wo_a", wo_bf[:, : 4 * 256], 256, "tab1", 0),
+            quantize("wo_b", wo_bf[:, 4 * 256 :], 128, "tab1", 1024),
+        ]
         wo_tiles = [(wo_q[0], 0), (wo_q[0], P), (wo_q[1], 0)]
-        s0 = 0
-        for width in STORES:
-            state = tile("state%d" % s0, [P, 3, width], F32)
-            for u0 in range(0, width, UNIT):
-                if s0 + u0 + UNIT < S:
-                    made.append(product(s0 + u0 + UNIT, UNIT))
-                project(s0 + u0, made[(s0 + u0) // UNIT], state[:, :, u0 : u0 + UNIT])
-            queue = nc.scalar if s0 + width == S else nc.sync
-            queue.dma_start(out=out_rows[:, :, s0 : s0 + width], in_=state[:])
+        k = 0
+        for store in STORES:
+            s0 = starts[k]
+            state = tile("state%d" % s0, [P, 3, sum(store)], F32)
+            for width in store:
+                if k + 1 < len(widths):
+                    made.append(product(starts[k + 1], widths[k + 1]))
+                u0 = starts[k] - s0
+                project(k, starts[k], width, made[k], state[:, :, u0 : u0 + width])
+                k = k + 1
+            queue = nc.scalar if k == len(widths) else nc.sync
+            queue.dma_start(out=out_rows[:, :, s0 : s0 + sum(store)], in_=state[:])
             if s0 == 0:
                 squash(last_banks, CHUNK, CHUNK)
-            s0 = s0 + width

@@ -25,7 +25,7 @@ UNIT = 128
 PAGE, TOKEN, PRED = 0, 1, 2
 LOAD = 8192
 LOADS = ("wt_raw", "tab0", "tab1", "wp_raw0", "wr_raw1", "wp_raw1", "wr_raw0", "wo_raw", "spare")
-STORES = ((128, 128), (128, 128), (128, 128), (128,), (128,))
+STORES = ((256,), (256,), (128, 128), (128,), (128,))
 
 
 def tile_list_paged_memory_cell_kernel(
@@ -74,7 +74,7 @@ def tile_list_paged_memory_cell_kernel(
             return rows
 
         lists = [load_list(name, src) for name, src in (("page", offs), ("token", offs2), ("pred", offs3))]
-        for q in range(4):
+        for q in (2, 3, 0, 1):
             nc.sync.dma_start(
                 out=tab_sc[32 * q : 32 * q + 8, :].bitcast(I32),
                 in_=tab_scales[:, 4 * q : 4 * q + 4, :].bitcast(I32),
@@ -170,9 +170,14 @@ def tile_list_paged_memory_cell_kernel(
             gate = tile("gate%d" % half, [P, 4, HALF], F32, "spare" if half else None)
             for t in range(4):
                 nc.scalar.activation(out=sig[:, t, :], in_=banks[t][:], func=ACT.Sigmoid)
-            for t in range(4):
+            on_gpsimd = 3 if half else 4
+            for t in range(on_gpsimd):
                 nc.gpsimd.tensor_scalar(
                     out=gate[:, t, :], in0=sig[:, t, :], scalar1=gain[:, 4 * t : 4 * t + 1], scalar2=0.0, op0=MULT, op1=ADD
+                )
+            for t in range(on_gpsimd, 4):
+                nc.scalar.activation(
+                    out=gate[:, t, :], in_=sig[:, t, :], func=ACT.Copy, scale=gain[:, 4 * t : 4 * t + 1]
                 )
             gates.append(gate)
 
@@ -249,21 +254,24 @@ def tile_list_paged_memory_cell_kernel(
 
         def project(k, s0, width, h_bf, state):
             h_codes, h_scales = quantize("h%d" % s0, h_bf[:], width)
-            dst = bank(k % 8)
-            for nt in range(3):
-                (codes, scales), m0 = wo_tiles[nt]
-                nc.tensor.matmul_mx(
-                    out=dst[:, nt * width : (nt + 1) * width],
-                    lhsT=codes[:, m0 : m0 + P].bitcast(FP8X4),
-                    lhsT_scale=scales[:, m0 : m0 + P],
-                    rhs=h_codes[:].bitcast(FP8X4),
-                    rhs_scale=h_scales[:],
-                    start=True,
-                    stop=True,
+            for u0 in range(0, width, UNIT):
+                dst = bank((s0 + u0) // UNIT)
+                for nt in range(3):
+                    (codes, scales), m0 = wo_tiles[nt]
+                    nc.tensor.matmul_mx(
+                        out=dst[:, nt * UNIT : (nt + 1) * UNIT],
+                        lhsT=codes[:, m0 : m0 + P].bitcast(FP8X4),
+                        lhsT_scale=scales[:, m0 : m0 + P],
+                        rhs=h_codes[:, u0 : u0 + UNIT].bitcast(FP8X4),
+                        rhs_scale=h_scales[:, u0 : u0 + UNIT],
+                        start=True,
+                        stop=True,
+                    )
+                nc.scalar.activation(
+                    out=state[:, :, u0 : u0 + UNIT],
+                    in_=dst[:, : 3 * UNIT].rearrange("p (nt s) -> p nt s", nt=3),
+                    func=ACT.Tanh,
                 )
-            nc.scalar.activation(
-                out=state, in_=dst[:, : 3 * width].rearrange("p (nt s) -> p nt s", nt=3), func=ACT.Tanh
-            )
 
         widths = [width for store in STORES for width in store]
         starts = [sum(widths[:k]) for k in range(len(widths))]

@@ -23,9 +23,10 @@ HALF = 512
 CHUNK = 256
 UNIT = 128
 PAGE, TOKEN, PRED = 0, 1, 2
-LOAD = 8192
-LOADS = ("wt_raw", "tab0", "tab1", "wp_raw0", "wr_raw1", "wp_raw1", "wr_raw0", "wo_raw", "spare")
-STORES = ((256,), (256,), (128, 128), (128,), (128,))
+A, B, C, D = 0, 1, 2, 3
+KIB = 1024
+PLACES = ("wp_raw0", "wp_raw1", "tab0", "wr_raw0", "tab1", "wr_raw1", "spare", "wo_raw", "small", "stage")
+PLACE = 8 * KIB
 
 
 def tile_list_paged_memory_cell_kernel(
@@ -35,12 +36,11 @@ def tile_list_paged_memory_cell_kernel(
     with ExitStack() as ctx:
         keep = ctx.enter_context(tc.tile_pool(name="keep", bufs=1))
         psum = ctx.enter_context(tc.psum_pool(name="psum", bufs=1))
-
         front = ctx.enter_context(tc.tile_pool(name="front", bufs=1))
 
-        def tile(name, shape, dtype, slot=None, at=0):
-            if name in LOADS or slot in LOADS:
-                return front.tile(shape, dtype, name=name, offset=LOADS.index(slot or name) * LOAD + at, align_bytes=64)
+        def tile(name, shape, dtype, place=None, at=0):
+            if name in PLACES or place in PLACES:
+                return front.tile(shape, dtype, name=name, offset=PLACES.index(place or name) * PLACE + at, align_bytes=64)
             return keep.tile(shape, dtype, name=name, align_bytes=64)
 
         def bank(b):
@@ -48,14 +48,12 @@ def tile_list_paged_memory_cell_kernel(
 
         tab_sc = tile("tab_sc", [P, T], U8)
         nc.gpsimd.memset(tab_sc[:].bitcast(I32), 0)
-        zeros = front.tile([P, len(LOADS) * LOAD // 4], I32, name="zeros", offset=0, align_bytes=64)
+        zeros = front.tile([P, len(PLACES) * PLACE // 4], I32, name="zeros", offset=0, align_bytes=64)
         wt_sc_raw = tile("wt_sc_raw", [P, PASSES * H], U8)
-        tok_sc1 = tile("tok_sc1", [P, S], U8)
         warm = tile("warm", [P, 2], F32)
         nc.vector.memset(zeros[:, : PASSES * H // 4], 0)
         nc.gpsimd.memset(warm[:, 0:1], 0.0)
         nc.vector.tensor_copy(out=wt_sc_raw[:].bitcast(I32), in_=zeros[:, : PASSES * H // 4])
-        nc.gpsimd.memset(tok_sc1[:].bitcast(I32), 0)
         nc.scalar.activation(out=warm[:, 1:2], in_=warm[:, 0:1], func=ACT.Sigmoid)
 
         def load_list(name, src):
@@ -80,52 +78,70 @@ def tile_list_paged_memory_cell_kernel(
                 in_=tab_scales[:, 4 * q : 4 * q + 4, :].bitcast(I32),
             )
         wp_raw = [load_rows("wp_raw0", wp, 0)]
-        wp_raw.append(load_rows("wp_raw1", wp, 1))
+        tab = [load_table(0)]
         for q in range(4):
             nc.sync.dma_start(
                 out=wt_sc_raw[32 * q : 32 * q + 4, :].bitcast(I32).rearrange("r (a w) -> r a w", a=PASSES),
                 in_=wt_scales[:, 4 * q : 4 * q + 4, :].bitcast(I32).rearrange("a r w -> r a w"),
             )
-        tab = [load_table(0)]
-        wr_raw = [load_rows("wr_raw0", wr, 0)]
+        wp_raw.append(load_rows("wp_raw1", wp, 1))
         tab.append(load_table(1))
-        wt_raw = tile("wt_raw", [P, PASSES, H // 2], I32)
+        wt_raw = tile("wt_raw", [P, PASSES, H // 2], I32, "small")
         nc.sync.dma_start(out=wt_raw[:], in_=wt_words.bitcast(I32).rearrange("a p w -> p a w"))
+        wr_raw = [load_rows("wr_raw0", wr, 0)]
+        gain = tile("gain", [P, 13], F32, "small", 2 * KIB)
+        g_rows = g.rearrange("(c x) -> c x", x=16)
+        for i in range(4):
+            nc.sync.dma_start(out=gain[i:P:4, :], in_=g_rows[:, i : i + 13])
+        wr_raw.append(load_rows("wr_raw1", wr, 1))
         wo_raw = tile("wo_raw", [P, 4, N], F32)
         wo_rows = wo.rearrange("(c t i) n -> t c i n", t=4, i=4)
         for t in range(4):
             nc.sync.dma_start(out=wo_raw[:, t, :], in_=wo_rows[t])
-        wr_raw.append(load_rows("wr_raw1", wr, 1))
 
-        def gather(name, window, n, s0, count, dtype, slot=None, at=0):
-            picked = tile(name, [P, count], dtype, slot, at)
+        def gather(name, window, n, s0, count, dtype, place=None, at=0):
+            picked = tile(name, [P, count], dtype, place, at)
             nc.vector.tensor_copy(picked[:], window.indirect(lists[n][:, s0 // 16 : (s0 + count) // 16]))
             return picked
 
-        def gather_scales(n, s0, count, slot=None, at=0):
-            return gather("sc%d_%d" % (n, s0), tab_sc[:], n, s0, count, U8, slot, at)
+        def gather_scales(n, place=None, at=0):
+            return gather("sc%d" % n, tab_sc[:], n, 0, S, U8, place, at)
 
-        def gather_words(n, a, s0, count, slot=None, at=0):
-            return gather("w%d_%d_%d" % (n, a, s0), tab[a][:].bitcast(U32), n, s0, count, U32, slot, at)
+        words = {}
 
-        def round_on_scalar(grouped, raw, on_scalar):
-            dst = grouped[:].rearrange("p (t c i j) -> p t c j i", t=4, i=4, j=4)
+        def pick(n, a, chunk, chunks=1, place=None, at=0):
+            picked = gather(
+                "w%d_%d_%d" % (n, a, chunk), tab[a][:].bitcast(U32), n, chunk * CHUNK, chunks * CHUNK, U32, place, at
+            )
+            for c in range(chunks):
+                words[n, a, chunk + c] = picked[:, c * CHUNK : (c + 1) * CHUNK]
+
+        def round_on_scalar(grouped, raw, t0, t1):
+            dst = grouped[:].rearrange("p (t c i j) -> p t c j i", t=4, i=4, j=4)[:, t0:t1]
             src = raw[:].rearrange("p j (c t i) -> p t c j i", t=4, i=4)
-            nc.scalar.copy(out=dst[:, :on_scalar], in_=src[:, :on_scalar])
+            nc.scalar.copy(out=dst, in_=src[:, t0:t1])
 
-        def quantize(name, grouped, width, slot=None, at=0):
-            codes = tile(name + "_codes", [P, width], U32, slot, at)
+        def round_on_gpsimd(grouped, raw, t0, t1):
+            dst = grouped[:].rearrange("p (t c i j) -> p c t i j", t=4, i=4, j=4)[:, :, t0:t1]
+            src = raw[:].rearrange("p j (c t i) -> p c t i j", t=4, i=4)
+            nc.gpsimd.tensor_scalar(out=dst, in0=src[:, :, t0:t1], scalar1=1.0, scalar2=0.0, op0=MULT, op1=ADD)
+
+        def quantize(name, grouped, width, place=None, at=0):
+            codes = tile(name + "_codes", [P, width], U32, place, at)
             scales = tile(name + "_scales", [P, width], U8)
             nc.vector.quantize_mx(out=codes[:].bitcast(FP8X4), scales=scales[:], in_=grouped)
             return codes, scales
 
-        def fp8_pass(dst, t, weight, words, scales, start, stop):
-            m = slice(P * t, P * (t + 1))
+        def quantize_slots(name, grouped, width, place=None, at=0):
+            codes, scales = quantize(name, grouped, width, place, at)
+            return [(codes[:, m : m + P], scales[:, m : m + P]) for m in range(0, width, P)]
+
+        def fp8_pass(dst, t, weight, moving, scales, start, stop):
             nc.tensor.matmul_mx(
                 out=dst,
-                lhsT=weight[0][:, m].bitcast(FP8X4),
-                lhsT_scale=weight[1][:, m],
-                rhs=words.bitcast(FP8X4),
+                lhsT=weight[t][0].bitcast(FP8X4),
+                lhsT_scale=weight[t][1],
+                rhs=moving.bitcast(FP8X4),
                 rhs_scale=scales,
                 start=start,
                 stop=stop,
@@ -133,165 +149,181 @@ def tile_list_paged_memory_cell_kernel(
 
         wt_codes = tile("wt_codes", [P, PASSES * H // 2], I32)
         wt_sc = tile("wt_sc", [P, PASSES * H // 4], I32)
-        nc.gpsimd.tensor_copy(
-            out=wt_codes[:].rearrange("p (a t c w) -> p a t c w", a=PASSES, t=4, w=2),
-            in_=wt_raw[:].rearrange("p a (c t w) -> p a t c w", t=4, w=2),
-        )
+        wp_bf = [tile("wp_bf0", [P, 4 * H], BF16), tile("wp_bf1", [P, 4 * H], BF16, "stage")]
+        round_on_scalar(wp_bf[0], wp_raw[0], 0, 4)
+        round_on_scalar(wp_bf[1], wp_raw[1], 2, 4)
+        tok_sc0 = gather_scales(TOKEN)
+        tok_sc1 = tile("tok_sc1", [P, S], U8)
+        nc.gpsimd.dma_start(out=tok_sc1[0:100, :].bitcast(I32), in_=tok_sc0[4:104, :].bitcast(I32))
         nc.gpsimd.tensor_copy(
             out=wt_sc[:].rearrange("p (a t c) -> p a t c", a=PASSES, t=4),
             in_=wt_sc_raw[:].bitcast(I32).rearrange("p (a c t) -> p a t c", a=PASSES, t=4),
         )
-
-        wp_bf = [tile("wp_bf%d" % a, [P, 4 * H], BF16) for a in range(PASSES)]
-        wr_bf = [tile("wr_bf0", [P, 4 * H], BF16, "wt_raw", 2048), tile("wr_bf1", [P, 4 * H], BF16, "spare")]
-        for grouped, raw in ((wp_bf[0], wp_raw[0]), (wp_bf[1], wp_raw[1]), (wr_bf[0], wr_raw[0])):
-            round_on_scalar(grouped, raw, 4)
-        tok_sc0 = gather_scales(TOKEN, 0, S)
-        nc.gpsimd.dma_start(out=tok_sc1[0:100, :].bitcast(I32), in_=tok_sc0[4:104, :].bitcast(I32))
-        gain = tile("gain", [P, 13], F32, "wo_raw", 4 * 4 * N)
-        g_rows = g.rearrange("(c x) -> c x", x=16)
-        for i in range(4):
-            nc.gpsimd.dma_start(out=gain[i:P:4, :], in_=g_rows[:, i : i + 13])
-        page_sc = gather_scales(PAGE, 0, S)
-        pred_sc = gather_scales(PRED, 0, S)
-        wp_q = [quantize("wp%d" % a, wp_bf[a][:], H) for a in range(PASSES)]
-
-        words = {}
-        gates = []
-        cells = []
-
-        def page_half(half):
-            banks = [bank(4 * half + t) for t in range(4)]
-            cols = slice(half * HALF, (half + 1) * HALF)
-            for a in range(PASSES):
-                for t in range(4):
-                    fp8_pass(banks[t][:], t, wp_q[a], words[PAGE, a, half], page_sc[4 * a : P, cols], a == 0, a == 1)
-            sig = tile("sig%d" % half, [P, 4, HALF], F32, ("wp_raw1", "wp_raw0")[half], 64)
-            gate = tile("gate%d" % half, [P, 4, HALF], F32, "spare" if half else None)
-            for t in range(4):
-                nc.scalar.activation(out=sig[:, t, :], in_=banks[t][:], func=ACT.Sigmoid)
-            on_gpsimd = 3 if half else 4
-            for t in range(on_gpsimd):
-                nc.gpsimd.tensor_scalar(
-                    out=gate[:, t, :], in0=sig[:, t, :], scalar1=gain[:, 4 * t : 4 * t + 1], scalar2=0.0, op0=MULT, op1=ADD
-                )
-            for t in range(on_gpsimd, 4):
-                nc.scalar.activation(
-                    out=gate[:, t, :], in_=sig[:, t, :], func=ACT.Copy, scale=gain[:, 4 * t : 4 * t + 1]
-                )
-            gates.append(gate)
-
-        def cell_half(half):
-            banks = [bank(4 * half + t) for t in range(4)]
-            cols = slice(half * HALF, (half + 1) * HALF)
-            for n, a in ((TOKEN, 0), (PRED, 0), (TOKEN, 1), (PRED, 1)):
-                for t in range(4):
-                    if n == PRED:
-                        fp8_pass(banks[t][:], t, wr_q[a], words[n, a, half], pred_sc[4 * a : P, cols], False, a == 1)
-                        continue
-                    w0 = (4 * a + t) * (P // 2)
-                    c0 = (4 * a + t) * (P // 4)
-                    nc.tensor.matmul_mx(
-                        out=banks[t][:],
-                        lhsT=wt_codes[:, w0 : w0 + P // 2].bitcast(FP4X4),
-                        lhsT_scale=wt_sc[:, c0 : c0 + P // 4].bitcast(U8),
-                        rhs=words[n, a, half].bitcast(FP8X4),
-                        rhs_scale=(tok_sc0, tok_sc1)[a][:, cols],
-                        start=a == 0,
-                        stop=False,
-                    )
-            return banks
-
-        def squash(banks, s0, width):
-            cell = tile("cell%d" % len(cells), [P, 4, width], F32)
-            for t in range(4):
-                nc.scalar.activation(out=cell[:, t, :], in_=banks[t][:, s0 : s0 + width], func=ACT.Tanh)
-            cells.extend(cell[:, :, c0 : c0 + CHUNK] for c0 in range(0, width, CHUNK))
-
-        def pick(n, a, half, slot=None, at=0):
-            words[n, a, half] = gather_words(n, a, half * HALF, HALF, slot, at)[:]
-
-        pick(PAGE, 0, 0)
-        pick(PAGE, 0, 1)
-        pick(PRED, 0, 0)
-        wr_q = [quantize("wr0", wr_bf[0][:], H)]
-        pick(PAGE, 1, 0, "wr_raw0", 2048)
-        wo_bf = tile("wo_bf", [P, 4 * N], BF16)
-        nc.gpsimd.tensor_scalar(
-            out=wo_bf[:].rearrange("p (n t) -> p n t", t=4),
-            in0=wo_raw[:].rearrange("p t n -> p n t"),
-            scalar1=1.0, scalar2=0.0, op0=MULT, op1=ADD,
+        round_on_gpsimd(wp_bf[1], wp_raw[1], 0, 2)
+        nc.gpsimd.tensor_copy(
+            out=wt_codes[:].rearrange("p (a t c w) -> p a t c w", a=PASSES, t=4, w=2),
+            in_=wt_raw[:].rearrange("p a (c t w) -> p a t c w", t=4, w=2),
         )
-        page_half(0)
-        pick(PAGE, 1, 1, "wr_raw0", 4096)
-        round_on_scalar(wr_bf[1], wr_raw[1], 4)
-        page_half(1)
-        pick(TOKEN, 0, 0, "wt_raw", 2048 + 64)
-        pick(TOKEN, 1, 0, "wr_raw0", 6144)
-        pick(PRED, 1, 0, "wt_raw", 64)
-        pick(TOKEN, 0, 1, "wt_raw", 4096 + 64)
-        wr_q.append(quantize("wr1", wr_bf[1][:], H))
-        first_banks = cell_half(0)
-        for s0 in range(0, HALF, CHUNK):
-            squash(first_banks, s0, CHUNK)
-        for place, (n, a) in enumerate(((PRED, 0), (TOKEN, 1), (PRED, 1))):
-            pick(n, a, 1, "wr_raw1", 2048 * (place + 1))
-        last_banks = cell_half(1)
-        squash(last_banks, 0, CHUNK)
-        out_rows = out.rearrange("(nt p) s -> p nt s", p=P)
+        page_sc = gather_scales(PAGE)
+        wp_q = []
+        wr_q = []
 
-        def product(s0, width):
-            h_bf = tile("h_bf%d" % s0, [P, 4 * width], BF16)
+        def sums(first_bank, width):
+            if width == CHUNK:
+                return [(bank(first_bank + b), 0, CHUNK, (2 * b, 2 * b + 1)) for b in range(2)]
+            return [(bank(first_bank + b), b * UNIT, UNIT, (0, 1, 2, 3)) for b in range(2)]
+
+        def stage_pass(layout, chunk, n, a, first, last):
+            for dst, e0, width, slots in layout:
+                cols = slice(chunk * CHUNK + e0, chunk * CHUNK + e0 + width)
+                moving = words[n, a, chunk][:, e0 : e0 + width]
+                for k, t in enumerate(slots):
+                    part = dst[:, k * width : (k + 1) * width]
+                    start = first and k == 0
+                    stop = last and k == len(slots) - 1
+                    if n == PAGE:
+                        fp8_pass(part, t, wp_q[a], moving, page_sc[4 * a : P, cols], start, stop)
+                    elif n == PRED:
+                        fp8_pass(part, t, wr_q[a], moving, pred_sc[4 * a : P, cols], start, stop)
+                    else:
+                        w0 = (4 * a + t) * (P // 2)
+                        c0 = (4 * a + t) * (P // 4)
+                        nc.tensor.matmul_mx(
+                            out=part,
+                            lhsT=wt_codes[:, w0 : w0 + P // 2].bitcast(FP4X4),
+                            lhsT_scale=wt_sc[:, c0 : c0 + P // 4].bitcast(U8),
+                            rhs=moving.bitcast(FP8X4),
+                            rhs_scale=(tok_sc0, tok_sc1)[a][:, cols],
+                            start=start,
+                            stop=stop,
+                        )
+
+        def leave(result, c0, layout, func):
+            for dst, e0, width, slots in layout:
+                nc.scalar.activation(
+                    out=result[:, slots[0] : slots[-1] + 1, c0 + e0 : c0 + e0 + width],
+                    in_=dst[:].rearrange("p (t e) -> p t e", e=width),
+                    func=func,
+                )
+
+        def squash(chunk):
+            result = tile("cell%d" % chunk, [P, 4, CHUNK], F32)
+            leave(result, 0, cell[chunk], ACT.Tanh)
+            return result
+
+        def apply_gain_on_gpsimd(gate, sig, t):
+            nc.gpsimd.tensor_scalar(
+                out=gate[:, t, :], in0=sig[:, t, :], scalar1=gain[:, 4 * t : 4 * t + 1], scalar2=0.0, op0=MULT, op1=ADD
+            )
+
+        def apply_gain(gate, sig, slots):
+            for t in slots:
+                nc.scalar.activation(out=gate[:, t, :], in_=sig[:, t, :], func=ACT.Copy, scale=gain[:, 4 * t : 4 * t + 1])
+
+        def product(engine, walk, s0, width, place=None):
+            h_bf = tile("h_bf%d" % s0, [P, 4 * width], BF16, place)
             gate = gates[s0 // HALF][:, :, s0 % HALF : s0 % HALF + width]
-            cell = cells[s0 // CHUNK][:, :, s0 % CHUNK : s0 % CHUNK + width]
-            nc.vector.tensor_tensor(
-                out=h_bf[:].rearrange("p (c i t) -> p c t i", t=4, i=4),
-                in0=gate.rearrange("p t (c i) -> p c t i", i=4),
-                in1=cell.rearrange("p t (c i) -> p c t i", i=4),
+            state = cells[s0 // CHUNK][:, :, s0 % CHUNK : s0 % CHUNK + width]
+            engine.tensor_tensor(
+                out=h_bf[:].rearrange("p (c i t) -> " + walk, t=4, i=4),
+                in0=gate.rearrange("p t (c i) -> " + walk, i=4),
+                in1=state.rearrange("p t (c i) -> " + walk, i=4),
                 op=MULT,
             )
             return h_bf
 
-        def project(k, s0, width, h_bf, state):
+        out_rows = out.rearrange("(nt p) s -> p nt s", p=P)
+
+        def project(s0, width, h_bf, queue):
             h_codes, h_scales = quantize("h%d" % s0, h_bf[:], width)
+            state = tile("state%d" % s0, [P, 3, width], F32)
             for u0 in range(0, width, UNIT):
                 dst = bank((s0 + u0) // UNIT)
                 for nt in range(3):
-                    (codes, scales), m0 = wo_tiles[nt]
-                    nc.tensor.matmul_mx(
-                        out=dst[:, nt * UNIT : (nt + 1) * UNIT],
-                        lhsT=codes[:, m0 : m0 + P].bitcast(FP8X4),
-                        lhsT_scale=scales[:, m0 : m0 + P],
-                        rhs=h_codes[:, u0 : u0 + UNIT].bitcast(FP8X4),
-                        rhs_scale=h_scales[:, u0 : u0 + UNIT],
-                        start=True,
-                        stop=True,
+                    fp8_pass(
+                        dst[:, nt * UNIT : (nt + 1) * UNIT], nt, wo_q, h_codes[:, u0 : u0 + UNIT],
+                        h_scales[:, u0 : u0 + UNIT], True, True,
                     )
                 nc.scalar.activation(
                     out=state[:, :, u0 : u0 + UNIT],
                     in_=dst[:, : 3 * UNIT].rearrange("p (nt s) -> p nt s", nt=3),
                     func=ACT.Tanh,
                 )
+            queue.dma_start(out=out_rows[:, :, s0 : s0 + width], in_=state[:])
 
-        widths = [width for store in STORES for width in store]
-        starts = [sum(widths[:k]) for k in range(len(widths))]
-        made = [product(0, widths[0])]
-        wo_q = [
-            quantize("wo_a", wo_bf[:, : 4 * 256], 256, "tab1", 0),
-            quantize("wo_b", wo_bf[:, 4 * 256 :], 128, "tab1", 1024),
-        ]
-        wo_tiles = [(wo_q[0], 0), (wo_q[0], P), (wo_q[1], 0)]
-        k = 0
-        for store in STORES:
-            s0 = starts[k]
-            state = tile("state%d" % s0, [P, 3, sum(store)], F32)
-            for width in store:
-                if k + 1 < len(widths):
-                    made.append(product(starts[k + 1], widths[k + 1]))
-                u0 = starts[k] - s0
-                project(k, starts[k], width, made[k], state[:, :, u0 : u0 + width])
-                k = k + 1
-            queue = nc.scalar if k == len(widths) else nc.sync
-            queue.dma_start(out=out_rows[:, :, s0 : s0 + sum(store)], in_=state[:])
-            if s0 == 0:
-                squash(last_banks, CHUNK, CHUNK)
+        page = {chunk: sums(2 * chunk, CHUNK) for chunk in (A, B, C, D)}
+        pick(PAGE, 0, A, 2)
+        wp_q.append(quantize_slots("wp0", wp_bf[0][:], H))
+        pick(PAGE, 0, C, 2, "wp_raw0", 0)
+        for chunk in (A, B, C, D):
+            stage_pass(page[chunk], chunk, PAGE, 0, True, False)
+        pick(TOKEN, 0, A, 2, "wp_raw0", 2 * KIB)
+        wp_q.append(quantize_slots("wp1", wp_bf[1][:], H))
+        pick(PAGE, 1, A, 2, "wp_raw1", 0)
+        sigs = [tile("sig0", [P, 4, HALF], F32)]
+        for chunk in (A, B):
+            stage_pass(page[chunk], chunk, PAGE, 1, False, True)
+            leave(sigs[0], chunk * CHUNK, page[chunk], ACT.Sigmoid)
+        pred_sc = gather_scales(PRED, "wp_raw1", 5 * KIB)
+        pick(PRED, 0, A, 2, "wp_raw1", 6 * KIB)
+        wr_bf = [tile("wr_bf0", [P, 4 * H], BF16, "stage")]
+        round_on_gpsimd(wr_bf[0], wr_raw[0], 0, 4)
+        wr_q.append(quantize_slots("wr0", wr_bf[0][:], H))
+        gates = [tile("gate0", [P, 4, HALF], F32)]
+        apply_gain(gates[0], sigs[0], (0, 1))
+        wr_bf.append(tile("wr_bf1", [P, 4 * H], BF16, "stage"))
+        round_on_gpsimd(wr_bf[1], wr_raw[1], 0, 2)
+        round_on_scalar(wr_bf[1], wr_raw[1], 2, 4)
+        apply_gain(gates[0], sigs[0], (2, 3))
+        cell = {A: sums(0, CHUNK), B: sums(2, CHUNK)}
+        stage_pass(cell[A], A, TOKEN, 0, True, False)
+        stage_pass(cell[B], B, TOKEN, 0, True, False)
+        stage_pass(cell[A], A, PRED, 0, False, False)
+        stage_pass(cell[B], B, PRED, 0, False, False)
+        pick(PAGE, 1, C, 2, "wr_raw0", KIB)
+        for chunk in (C, D):
+            stage_pass(page[chunk], chunk, PAGE, 1, False, True)
+        pick(PRED, 1, A, 1, "wr_raw0")
+        wr_q.append(quantize_slots("wr1", wr_bf[1][:], H))
+        stage_pass(cell[A], A, PRED, 1, False, False)
+        pick(TOKEN, 1, A, 1, "wr_raw1")
+        stage_pass(cell[A], A, TOKEN, 1, False, True)
+        cells = [squash(A)]
+        sigs.append(tile("sig1", [P, 4, HALF], F32, "wr_raw1", 7 * KIB))
+        for chunk in (C, D):
+            leave(sigs[1], (chunk - C) * CHUNK, page[chunk], ACT.Sigmoid)
+        wo_bf = tile("wo_bf", [P, 4 * N], BF16, "stage", 2 * KIB)
+        nc.gpsimd.tensor_scalar(
+            out=wo_bf[:].rearrange("p (n t) -> p n t", t=4),
+            in0=wo_raw[:].rearrange("p t n -> p n t"),
+            scalar1=1.0, scalar2=0.0, op0=MULT, op1=ADD,
+        )
+        gates.append(tile("gate1", [P, 4, HALF], F32))
+        apply_gain_on_gpsimd(gates[1], sigs[1], 0)
+        made = {0: product(nc.gpsimd, "p c i t", 0, CHUNK)}
+
+        cell[C] = sums(4, CHUNK)
+        for k, n in enumerate((TOKEN, PRED)):
+            pick(n, 1, B, 2, "wr_raw1", (1 + 2 * k) * KIB)
+            stage_pass(cell[B], B, n, 1, False, k == 1)
+            stage_pass(cell[C], C, n, 1, k == 0, False)
+        cells.append(squash(B))
+        cell[D] = sums(6, UNIT)
+        for k, n in enumerate((TOKEN, PRED)):
+            pick(n, 0, C, 2, ("wr_raw1", "stage")[k], (5 * KIB, 0)[k])
+            stage_pass(cell[C], C, n, 0, False, k == 1)
+            stage_pass(cell[D], D, n, 0, k == 0, False)
+        cells.append(squash(C))
+        apply_gain(gates[1], sigs[1], (1, 2, 3))
+        for k, n in enumerate((TOKEN, PRED)):
+            pick(n, 1, D, 1, ("wr_raw1", "wr_raw0")[k])
+            stage_pass(cell[D], D, n, 1, False, k == 1)
+        cells.append(squash(D))
+
+        steps = ((0, CHUNK), (CHUNK, CHUNK), (2 * CHUNK, UNIT), (5 * UNIT, UNIT), (6 * UNIT, UNIT), (7 * UNIT, UNIT))
+        made[CHUNK] = product(nc.vector, "p c t i", CHUNK, CHUNK, "tab0")
+        wo_q = quantize_slots("wo", wo_bf[:], N, "tab1")
+        for k, (s0, width) in enumerate(steps):
+            if 0 < k < len(steps) - 1:
+                made[steps[k + 1][0]] = product(nc.vector, "p c t i", steps[k + 1][0], steps[k + 1][1])
+            project(s0, width, made[s0], nc.scalar if k == len(steps) - 1 else nc.sync)

@@ -300,7 +300,7 @@ def tile_list_paged_memory_cell_kernel(
         )
         gates.append(tile("gate1", [P, 4, HALF], F32))
         apply_gain_on_gpsimd(gates[1], sigs[1], 0)
-        made = {0: product(nc.gpsimd, "p c i t", 0, CHUNK)}
+        made = {0: product(nc.gpsimd, "p c t i", 0, CHUNK)}
 
         cell[C] = sums(4, CHUNK)
         for k, n in enumerate((TOKEN, PRED)):

@@ -147,11 +147,10 @@ def tile_list_paged_memory_cell_kernel(
                 stop=stop,
             )
 
-        wt_codes = tile("wt_codes", [P, PASSES * H // 2], I32)
         wt_sc = tile("wt_sc", [P, PASSES * H // 4], I32)
-        wp_bf = [tile("wp_bf0", [P, 4 * H], BF16), tile("wp_bf1", [P, 4 * H], BF16, "stage")]
+        wp_bf = [tile("wp_bf0", [P, 4 * H], BF16, "stage", 3 * KIB)]
+        wp_q = []
         round_on_scalar(wp_bf[0], wp_raw[0], 0, 4)
-        round_on_scalar(wp_bf[1], wp_raw[1], 2, 4)
         tok_sc0 = gather_scales(TOKEN)
         tok_sc1 = tile("tok_sc1", [P, S], U8)
         nc.gpsimd.dma_start(out=tok_sc1[0:100, :].bitcast(I32), in_=tok_sc0[4:104, :].bitcast(I32))
@@ -159,13 +158,7 @@ def tile_list_paged_memory_cell_kernel(
             out=wt_sc[:].rearrange("p (a t c) -> p a t c", a=PASSES, t=4),
             in_=wt_sc_raw[:].bitcast(I32).rearrange("p (a c t) -> p a t c", a=PASSES, t=4),
         )
-        round_on_gpsimd(wp_bf[1], wp_raw[1], 0, 2)
-        nc.gpsimd.tensor_copy(
-            out=wt_codes[:].rearrange("p (a t c w) -> p a t c w", a=PASSES, t=4, w=2),
-            in_=wt_raw[:].rearrange("p a (c t w) -> p a t c w", t=4, w=2),
-        )
         page_sc = gather_scales(PAGE)
-        wp_q = []
         wr_q = []
 
         def sums(first_bank, width):
@@ -254,11 +247,19 @@ def tile_list_paged_memory_cell_kernel(
         page = {chunk: sums(2 * chunk, CHUNK) for chunk in (A, B, C, D)}
         pick(PAGE, 0, A, 2)
         wp_q.append(quantize_slots("wp0", wp_bf[0][:], H))
+        wp_bf.append(tile("wp_bf1", [P, 4 * H], BF16, "stage", 3 * KIB))
+        round_on_scalar(wp_bf[1], wp_raw[1], 2, 4)
+        round_on_gpsimd(wp_bf[1], wp_raw[1], 0, 2)
         pick(PAGE, 0, C, 2, "wp_raw0", 0)
         for chunk in (A, B, C, D):
             stage_pass(page[chunk], chunk, PAGE, 0, True, False)
         pick(TOKEN, 0, A, 2, "wp_raw0", 2 * KIB)
         wp_q.append(quantize_slots("wp1", wp_bf[1][:], H))
+        wt_codes = tile("wt_codes", [P, PASSES * H // 2], I32, "stage", 5 * KIB)
+        nc.gpsimd.tensor_copy(
+            out=wt_codes[:].rearrange("p (a t c w) -> p a t c w", a=PASSES, t=4, w=2),
+            in_=wt_raw[:].rearrange("p a (c t w) -> p a t c w", t=4, w=2),
+        )
         pick(PAGE, 1, A, 2, "wp_raw1", 0)
         sigs = [tile("sig0", [P, 4, HALF], F32)]
         for chunk in (A, B):
@@ -266,12 +267,12 @@ def tile_list_paged_memory_cell_kernel(
             leave(sigs[0], chunk * CHUNK, page[chunk], ACT.Sigmoid)
         pred_sc = gather_scales(PRED, "wp_raw1", 5 * KIB)
         pick(PRED, 0, A, 2, "wp_raw1", 6 * KIB)
-        wr_bf = [tile("wr_bf0", [P, 4 * H], BF16, "stage")]
+        wr_bf = [tile("wr_bf0", [P, 4 * H], BF16, "stage", KIB)]
         round_on_gpsimd(wr_bf[0], wr_raw[0], 0, 4)
         wr_q.append(quantize_slots("wr0", wr_bf[0][:], H))
         gates = [tile("gate0", [P, 4, HALF], F32)]
         apply_gain(gates[0], sigs[0], (0, 1))
-        wr_bf.append(tile("wr_bf1", [P, 4 * H], BF16, "stage"))
+        wr_bf.append(tile("wr_bf1", [P, 4 * H], BF16, "stage", KIB))
         round_on_gpsimd(wr_bf[1], wr_raw[1], 0, 2)
         round_on_scalar(wr_bf[1], wr_raw[1], 2, 4)
         apply_gain(gates[0], sigs[0], (2, 3))
@@ -292,7 +293,7 @@ def tile_list_paged_memory_cell_kernel(
         sigs.append(tile("sig1", [P, 4, HALF], F32, "wr_raw1", 7 * KIB))
         for chunk in (C, D):
             leave(sigs[1], (chunk - C) * CHUNK, page[chunk], ACT.Sigmoid)
-        wo_bf = tile("wo_bf", [P, 4 * N], BF16, "stage", 2 * KIB)
+        wo_bf = tile("wo_bf", [P, 4 * N], BF16, "stage")
         nc.gpsimd.tensor_scalar(
             out=wo_bf[:].rearrange("p (n t) -> p n t", t=4),
             in0=wo_raw[:].rearrange("p t n -> p n t"),
@@ -310,7 +311,7 @@ def tile_list_paged_memory_cell_kernel(
         cells.append(squash(B))
         cell[D] = sums(6, UNIT)
         for k, n in enumerate((TOKEN, PRED)):
-            pick(n, 0, C, 2, ("wr_raw1", "stage")[k], (5 * KIB, 0)[k])
+            pick(n, 0, C, 2, ("wr_raw1", "stage")[k], (5 * KIB, 3 * KIB)[k])
             stage_pass(cell[C], C, n, 0, False, k == 1)
             stage_pass(cell[D], D, n, 0, k == 0, False)
         cells.append(squash(C))

@@ -25,7 +25,7 @@ UNIT = 128
 PAGE, TOKEN, PRED = 0, 1, 2
 A, B, C, D = 0, 1, 2, 3
 KIB = 1024
-PLACES = ("wp_raw0", "wp_raw1", "tab0", "wr_raw0", "tab1", "wr_raw1", "spare", "wo_raw", "small", "stage")
+PLACES = ("wp_raw0", "wp_raw1", "late", "tab0", "tab1", "wr_raw0", "wr_raw1", "spare", "wo_raw", "small", "stage")
 PLACE = 8 * KIB
 
 
@@ -260,40 +260,40 @@ def tile_list_paged_memory_cell_kernel(
             out=wt_codes[:].rearrange("p (a t c w) -> p a t c w", a=PASSES, t=4, w=2),
             in_=wt_raw[:].rearrange("p a (c t w) -> p a t c w", t=4, w=2),
         )
-        pick(PAGE, 1, A, 2, "wp_raw1", 0)
+        pick(PAGE, 1, A, 2, "wp_raw1", 7 * KIB)
         sigs = [tile("sig0", [P, 4, HALF], F32)]
         for chunk in (A, B):
             stage_pass(page[chunk], chunk, PAGE, 1, False, True)
             leave(sigs[0], chunk * CHUNK, page[chunk], ACT.Sigmoid)
-        pred_sc = gather_scales(PRED, "wp_raw1", 5 * KIB)
-        pick(PRED, 0, A, 2, "wp_raw1", 6 * KIB)
+        pred_sc = gather_scales(PRED, "wp_raw1")
+        pick(PRED, 0, A, 2, "wp_raw1", KIB)
         wr_bf = [tile("wr_bf0", [P, 4 * H], BF16, "stage", KIB)]
         round_on_gpsimd(wr_bf[0], wr_raw[0], 0, 4)
-        wr_q.append(quantize_slots("wr0", wr_bf[0][:], H))
         gates = [tile("gate0", [P, 4, HALF], F32)]
         apply_gain(gates[0], sigs[0], (0, 1))
-        wr_bf.append(tile("wr_bf1", [P, 4 * H], BF16, "stage", KIB))
+        wr_bf.append(tile("wr_bf1", [P, 4 * H], BF16, "late"))
         round_on_gpsimd(wr_bf[1], wr_raw[1], 0, 2)
         round_on_scalar(wr_bf[1], wr_raw[1], 2, 4)
         apply_gain(gates[0], sigs[0], (2, 3))
         cell = {A: sums(0, CHUNK), B: sums(2, CHUNK)}
         stage_pass(cell[A], A, TOKEN, 0, True, False)
         stage_pass(cell[B], B, TOKEN, 0, True, False)
-        stage_pass(cell[A], A, PRED, 0, False, False)
-        stage_pass(cell[B], B, PRED, 0, False, False)
-        pick(PAGE, 1, C, 2, "wr_raw0", KIB)
+        pick(PAGE, 1, C, 2, "wp_raw0", KIB)
         for chunk in (C, D):
             stage_pass(page[chunk], chunk, PAGE, 1, False, True)
-        pick(PRED, 1, A, 1, "wr_raw0")
+        pick(PRED, 1, A, 1, "wp_raw1", 3 * KIB)
+        pick(TOKEN, 1, A, 1, "wp_raw0", 3 * KIB)
+        stage_pass(cell[A], A, TOKEN, 1, False, False)
+        wr_q.append(quantize_slots("wr0", wr_bf[0][:], H, "wr_raw0", 7 * KIB))
         wr_q.append(quantize_slots("wr1", wr_bf[1][:], H))
-        stage_pass(cell[A], A, PRED, 1, False, False)
-        pick(TOKEN, 1, A, 1, "wr_raw1")
-        stage_pass(cell[A], A, TOKEN, 1, False, True)
+        stage_pass(cell[A], A, PRED, 0, False, False)
+        stage_pass(cell[A], A, PRED, 1, False, True)
+        stage_pass(cell[B], B, PRED, 0, False, False)
         cells = [squash(A)]
         sigs.append(tile("sig1", [P, 4, HALF], F32, "wr_raw1", 7 * KIB))
         for chunk in (C, D):
             leave(sigs[1], (chunk - C) * CHUNK, page[chunk], ACT.Sigmoid)
-        wo_bf = tile("wo_bf", [P, 4 * N], BF16, "stage")
+        wo_bf = tile("wo_bf", [P, 4 * N], BF16, "late", 2 * KIB)
         nc.gpsimd.tensor_scalar(
             out=wo_bf[:].rearrange("p (n t) -> p n t", t=4),
             in0=wo_raw[:].rearrange("p t n -> p n t"),
@@ -311,13 +311,13 @@ def tile_list_paged_memory_cell_kernel(
         cells.append(squash(B))
         cell[D] = sums(6, UNIT)
         for k, n in enumerate((TOKEN, PRED)):
-            pick(n, 0, C, 2, ("wr_raw1", "stage")[k], (5 * KIB, 3 * KIB)[k])
+            pick(n, 0, C, 2, ("wr_raw1", "late")[k], (5 * KIB, 0)[k])
             stage_pass(cell[C], C, n, 0, False, k == 1)
             stage_pass(cell[D], D, n, 0, k == 0, False)
         cells.append(squash(C))
         apply_gain(gates[1], sigs[1], (1, 2, 3))
         for k, n in enumerate((TOKEN, PRED)):
-            pick(n, 1, D, 1, ("wr_raw1", "wr_raw0")[k])
+            pick(n, 1, D, 1, "wp_raw1", 2 * KIB + 512 + k * KIB)
             stage_pass(cell[D], D, n, 1, False, k == 1)
         cells.append(squash(D))
 

@@ -204,11 +204,6 @@ def tile_list_paged_memory_cell_kernel(
             leave(result, 0, cell[chunk], ACT.Tanh)
             return result
 
-        def apply_gain_on_gpsimd(gate, sig, t):
-            nc.gpsimd.tensor_scalar(
-                out=gate[:, t, :], in0=sig[:, t, :], scalar1=gain[:, 4 * t : 4 * t + 1], scalar2=0.0, op0=MULT, op1=ADD
-            )
-
         def apply_gain(gate, sig, slots):
             for t in slots:
                 nc.scalar.activation(out=gate[:, t, :], in_=sig[:, t, :], func=ACT.Copy, scale=gain[:, 4 * t : 4 * t + 1])
@@ -265,8 +260,10 @@ def tile_list_paged_memory_cell_kernel(
         for chunk in (A, B):
             stage_pass(page[chunk], chunk, PAGE, 1, False, True)
             leave(sigs[0], chunk * CHUNK, page[chunk], ACT.Sigmoid)
+        pick(PAGE, 1, C, 2, "wp_raw1", KIB)
+        for chunk in (C, D):
+            stage_pass(page[chunk], chunk, PAGE, 1, False, True)
         pred_sc = gather_scales(PRED, "wp_raw1")
-        pick(PRED, 0, A, 2, "wp_raw1", KIB)
         wr_bf = [tile("wr_bf0", [P, 4 * H], BF16, "stage", KIB)]
         round_on_gpsimd(wr_bf[0], wr_raw[0], 0, 4)
         gates = [tile("gate0", [P, 4, HALF], F32)]
@@ -278,35 +275,33 @@ def tile_list_paged_memory_cell_kernel(
         cell = {A: sums(0, CHUNK), B: sums(2, CHUNK)}
         stage_pass(cell[A], A, TOKEN, 0, True, False)
         stage_pass(cell[B], B, TOKEN, 0, True, False)
-        pick(PAGE, 1, C, 2, "wp_raw0", KIB)
-        for chunk in (C, D):
-            stage_pass(page[chunk], chunk, PAGE, 1, False, True)
         pick(PRED, 1, A, 1, "wp_raw1", 3 * KIB)
         pick(TOKEN, 1, A, 1, "wp_raw0", 3 * KIB)
         stage_pass(cell[A], A, TOKEN, 1, False, False)
+        pick(PRED, 0, A, 2, "wp_raw0", KIB)
         wr_q.append(quantize_slots("wr0", wr_bf[0][:], H, "wr_raw0", 7 * KIB))
         wr_q.append(quantize_slots("wr1", wr_bf[1][:], H))
         stage_pass(cell[A], A, PRED, 0, False, False)
         stage_pass(cell[A], A, PRED, 1, False, True)
-        stage_pass(cell[B], B, PRED, 0, False, False)
         cells = [squash(A)]
         sigs.append(tile("sig1", [P, 4, HALF], F32, "wr_raw1", 7 * KIB))
         for chunk in (C, D):
             leave(sigs[1], (chunk - C) * CHUNK, page[chunk], ACT.Sigmoid)
         wo_bf = tile("wo_bf", [P, 4 * N], BF16, "late", 2 * KIB)
         nc.gpsimd.tensor_scalar(
-            out=wo_bf[:].rearrange("p (n t) -> p n t", t=4),
-            in0=wo_raw[:].rearrange("p t n -> p n t"),
+            out=wo_bf[:].rearrange("p (n t) -> p n t", t=4)[:, : 2 * P],
+            in0=wo_raw[:].rearrange("p t n -> p n t")[:, : 2 * P],
             scalar1=1.0, scalar2=0.0, op0=MULT, op1=ADD,
         )
         gates.append(tile("gate1", [P, 4, HALF], F32))
-        apply_gain_on_gpsimd(gates[1], sigs[1], 0)
         made = {0: product(nc.gpsimd, "p c t i", 0, CHUNK)}
 
         cell[C] = sums(4, CHUNK)
         for k, n in enumerate((TOKEN, PRED)):
             pick(n, 1, B, 2, "wr_raw1", (1 + 2 * k) * KIB)
             stage_pass(cell[B], B, n, 1, False, k == 1)
+            if n == TOKEN:
+                stage_pass(cell[B], B, PRED, 0, False, False)
             stage_pass(cell[C], C, n, 1, k == 0, False)
         cells.append(squash(B))
         cell[D] = sums(6, UNIT)
@@ -315,7 +310,11 @@ def tile_list_paged_memory_cell_kernel(
             stage_pass(cell[C], C, n, 0, False, k == 1)
             stage_pass(cell[D], D, n, 0, k == 0, False)
         cells.append(squash(C))
-        apply_gain(gates[1], sigs[1], (1, 2, 3))
+        nc.scalar.copy(
+            out=wo_bf[:].rearrange("p (c i t) -> p c t i", t=4, i=4)[:, P // 2 :],
+            in_=wo_raw[:].rearrange("p t (c i) -> p c t i", i=4)[:, P // 2 :],
+        )
+        apply_gain(gates[1], sigs[1], range(4))
         for k, n in enumerate((TOKEN, PRED)):
             pick(n, 1, D, 1, "wp_raw1", 2 * KIB + 512 + k * KIB)
             stage_pass(cell[D], D, n, 1, False, k == 1)

@@ -24,6 +24,7 @@ CHUNK = 256
 UNIT = 128
 PAGE, TOKEN, PRED = 0, 1, 2
 A, B, C, D = 0, 1, 2, 3
+STORES = ((CHUNK,), (UNIT, UNIT), (UNIT,), (UNIT,))
 KIB = 1024
 PLACES = ("wp_raw0", "wp_raw1", "late", "tab0", "tab1", "wr_raw0", "wr_raw1", "spare", "wo_raw", "small", "stage")
 PLACE = 8 * KIB
@@ -36,7 +37,6 @@ def tile_list_paged_memory_cell_kernel(
     with ExitStack() as ctx:
         keep = ctx.enter_context(tc.tile_pool(name="keep", bufs=1))
         psum = ctx.enter_context(tc.psum_pool(name="psum", bufs=1))
-        front = ctx.enter_context(tc.tile_pool(name="front", bufs=1))
 
         def tile(name, shape, dtype, place=None, at=0):
             if name in PLACES or place in PLACES:
@@ -48,12 +48,14 @@ def tile_list_paged_memory_cell_kernel(
 
         tab_sc = tile("tab_sc", [P, T], U8)
         nc.gpsimd.memset(tab_sc[:].bitcast(I32), 0)
-        zeros = front.tile([P, len(PLACES) * PLACE // 4], I32, name="zeros", offset=0, align_bytes=64)
         wt_sc_raw = tile("wt_sc_raw", [P, PASSES * H], U8)
         warm = tile("warm", [P, 2], F32)
-        nc.vector.memset(zeros[:, : PASSES * H // 4], 0)
         nc.gpsimd.memset(warm[:, 0:1], 0.0)
-        nc.vector.tensor_copy(out=wt_sc_raw[:].bitcast(I32), in_=zeros[:, : PASSES * H // 4])
+        with tc.tile_pool(name="boot", bufs=1) as boot:
+            zeros = boot.tile([P, PASSES * H // 4], I32, name="zeros")
+            nc.vector.memset(zeros[:], 0)
+            nc.vector.tensor_copy(out=wt_sc_raw[:].bitcast(I32), in_=zeros[:])
+        front = ctx.enter_context(tc.tile_pool(name="front", bufs=1))
         nc.scalar.activation(out=warm[:, 1:2], in_=warm[:, 0:1], func=ACT.Sigmoid)
 
         def load_list(name, src):
@@ -222,9 +224,11 @@ def tile_list_paged_memory_cell_kernel(
 
         out_rows = out.rearrange("(nt p) s -> p nt s", p=P)
 
-        def project(s0, width, h_bf, queue):
-            h_codes, h_scales = quantize("h%d" % s0, h_bf[:], width)
-            state = tile("state%d" % s0, [P, 3, width], F32)
+        def project(s0, width, h_bf, state):
+            project_codes(s0, 0, width, quantize("h%d" % s0, h_bf[:], width), state)
+
+        def project_codes(s0, c0, width, h_q, state):
+            h_codes, h_scales = h_q[0][:, c0:], h_q[1][:, c0:]
             for u0 in range(0, width, UNIT):
                 dst = bank((s0 + u0) // UNIT)
                 for nt in range(3):
@@ -237,7 +241,6 @@ def tile_list_paged_memory_cell_kernel(
                     in_=dst[:, : 3 * UNIT].rearrange("p (nt s) -> p nt s", nt=3),
                     func=ACT.Tanh,
                 )
-            queue.dma_start(out=out_rows[:, :, s0 : s0 + width], in_=state[:])
 
         page = {chunk: sums(2 * chunk, CHUNK) for chunk in (A, B, C, D)}
         pick(PAGE, 0, A, 2)
@@ -318,12 +321,23 @@ def tile_list_paged_memory_cell_kernel(
         for k, n in enumerate((TOKEN, PRED)):
             pick(n, 1, D, 1, "wp_raw1", 2 * KIB + 512 + k * KIB)
             stage_pass(cell[D], D, n, 1, False, k == 1)
-        cells.append(squash(D))
 
-        steps = ((0, CHUNK), (CHUNK, CHUNK), (2 * CHUNK, UNIT), (5 * UNIT, UNIT), (6 * UNIT, UNIT), (7 * UNIT, UNIT))
-        made[CHUNK] = product(nc.vector, "p c t i", CHUNK, CHUNK, "tab0")
-        wo_q = quantize_slots("wo", wo_bf[:], N, "tab1")
-        for k, (s0, width) in enumerate(steps):
-            if 0 < k < len(steps) - 1:
-                made[steps[k + 1][0]] = product(nc.vector, "p c t i", steps[k + 1][0], steps[k + 1][1])
-            project(s0, width, made[s0], nc.scalar if k == len(steps) - 1 else nc.sync)
+        wo_q = quantize_slots("wo", wo_bf[:], N, "tab0")
+        first_q = quantize("h0", made[0][:], CHUNK)
+        for s0 in range(0, CHUNK, UNIT):
+            state = tile("state%d" % s0, [P, 3, UNIT], F32)
+            project_codes(s0, s0, UNIT, first_q, state)
+            nc.sync.dma_start(out=out_rows[:, :, s0 : s0 + UNIT], in_=state[:])
+        cells.append(squash(D))
+        made[CHUNK] = product(nc.vector, "p c t i", CHUNK, CHUNK, "tab1")
+        s0 = CHUNK
+        for store in STORES:
+            first = s0
+            state = tile("state%d" % first, [P, 3, sum(store)], F32)
+            for width in store:
+                if s0 + width < S:
+                    made[s0 + width] = product(nc.vector, "p c t i", s0 + width, UNIT)
+                project(s0, width, made[s0], state[:, :, s0 - first : s0 - first + width])
+                s0 = s0 + width
+            queue = nc.sync if s0 < S else nc.scalar
+            queue.dma_start(out=out_rows[:, :, first:s0], in_=state[:])

@@ -47,7 +47,7 @@ def tile_list_paged_memory_cell_kernel(
             return psum.tile([P, 512], F32, name="bank%d" % b)
 
         tab_sc = tile("tab_sc", [P, T], U8)
-        nc.gpsimd.memset(tab_sc[:].bitcast(I32), 0)
+        nc.vector.memset(tab_sc[:].bitcast(I32), 0)
         wt_sc_raw = tile("wt_sc_raw", [P, PASSES * H], U8)
         warm = tile("warm", [P, 2], F32)
         nc.gpsimd.memset(warm[:, 0:1], 0.0)

@@ -50,13 +50,12 @@ def tile_list_paged_memory_cell_kernel(
         nc.vector.memset(tab_sc[:].bitcast(I32), 0)
         wt_sc_raw = tile("wt_sc_raw", [P, PASSES * H], U8)
         warm = tile("warm", [P, 2], F32)
-        nc.gpsimd.memset(warm[:, 0:1], 0.0)
+        nc.vector.memset(warm[:, 0:1], 0.0)
         with tc.tile_pool(name="boot", bufs=1) as boot:
             zeros = boot.tile([P, PASSES * H // 4], I32, name="zeros")
             nc.vector.memset(zeros[:], 0)
             nc.vector.tensor_copy(out=wt_sc_raw[:].bitcast(I32), in_=zeros[:])
         front = ctx.enter_context(tc.tile_pool(name="front", bufs=1))
-        nc.scalar.activation(out=warm[:, 1:2], in_=warm[:, 0:1], func=ACT.Sigmoid)
 
         def load_list(name, src):
             lst = tile(name, [P, S // 16], U16)
@@ -75,10 +74,11 @@ def tile_list_paged_memory_cell_kernel(
 
         lists = [load_list(name, src) for name, src in (("page", offs), ("token", offs2), ("pred", offs3))]
         for q in (2, 3, 0, 1):
-            nc.sync.dma_start(
+            (nc.scalar, nc.sync)[q // 2].dma_start(
                 out=tab_sc[32 * q : 32 * q + 8, :].bitcast(I32),
                 in_=tab_scales[:, 4 * q : 4 * q + 4, :].bitcast(I32),
             )
+        nc.scalar.activation(out=warm[:, 1:2], in_=warm[:, 0:1], func=ACT.Sigmoid)
         wp_raw = [load_rows("wp_raw0", wp, 0)]
         tab = [load_table(0)]
         for q in range(4):

from contextlib import ExitStack

import concourse.mybir as mybir

K, T, S, H, N = 1024, 2048, 1024, 512, 384
FLOPS = 2 * S * (3 * K * H + H * N)

F32 = mybir.dt.float32
BF16 = mybir.dt.bfloat16
I32 = mybir.dt.int32
U32 = mybir.dt.uint32
U16 = mybir.dt.uint16
U8 = mybir.dt.uint8
FP8X4 = mybir.dt.float8_e4m3fn_x4
FP4X4 = mybir.dt.float4_e2m1fn_x4
ACT = mybir.ActivationFunctionType
MULT = mybir.AluOpType.mult
ADD = mybir.AluOpType.add

P = 128
PASSES = K // 512
HALF = 512
CHUNK = 256
UNIT = 128
PAGE, TOKEN, PRED = 0, 1, 2
A, B, C, D = 0, 1, 2, 3
STORES = ((CHUNK,), (UNIT, UNIT), (UNIT,), (UNIT,))
KIB = 1024
PLACES = ("wp_raw0", "wp_raw1", "late", "tab0", "tab1", "wr_raw0", "wr_raw1", "spare", "wo_raw", "small", "stage")
PLACE = 8 * KIB


def tile_list_paged_memory_cell_kernel(
    tc, tab_words, tab_scales, offs, offs2, offs3, wp, wt_words, wt_scales, wr, g, wo, out
):
    nc = tc.nc
    with ExitStack() as ctx:
        keep = ctx.enter_context(tc.tile_pool(name="keep", bufs=1))
        psum = ctx.enter_context(tc.psum_pool(name="psum", bufs=1))

        def tile(name, shape, dtype, place=None, at=0):
            if name in PLACES or place in PLACES:
                return front.tile(shape, dtype, name=name, offset=PLACES.index(place or name) * PLACE + at, align_bytes=64)
            return keep.tile(shape, dtype, name=name, align_bytes=64)

        def bank(b):
            return psum.tile([P, 512], F32, name="bank%d" % b)

        tab_sc = tile("tab_sc", [P, T], U8)
        nc.vector.memset(tab_sc[:].bitcast(I32), 0)
        wt_sc_raw = tile("wt_sc_raw", [P, PASSES * H], U8)
        warm = tile("warm", [P, 2], F32)
        nc.vector.memset(warm[:, 0:1], 0.0)
        with tc.tile_pool(name="boot", bufs=1) as boot:
            zeros = boot.tile([P, PASSES * H // 4], I32, name="zeros")
            nc.vector.memset(zeros[:], 0)
            nc.vector.tensor_copy(out=wt_sc_raw[:].bitcast(I32), in_=zeros[:])
        front = ctx.enter_context(tc.tile_pool(name="front", bufs=1))

        def load_list(name, src):
            lst = tile(name, [P, S // 16], U16)
            nc.sync.dma_start(lst[:], src)
            return lst

        def load_table(a):
            words = tile("tab%d" % a, [P, T], I32)
            nc.sync.dma_start(out=words[:], in_=tab_words[a].rearrange("p t i -> p (t i)").bitcast(I32))
            return words

        def load_rows(name, w, a):
            rows = tile(name, [P, 4, H], F32)
            nc.sync.dma_start(out=rows[:], in_=w[512 * a : 512 * (a + 1), :].rearrange("(p j) r -> p j r", j=4))
            return rows

        lists = [load_list(name, src) for name, src in (("page", offs), ("token", offs2), ("pred", offs3))]
        for q in (2, 3, 0, 1):
            (nc.scalar, nc.sync)[q // 2].dma_start(
                out=tab_sc[32 * q : 32 * q + 8, :].bitcast(I32),
                in_=tab_scales[:, 4 * q : 4 * q + 4, :].bitcast(I32),
            )
        nc.scalar.activation(out=warm[:, 1:2], in_=warm[:, 0:1], func=ACT.Sigmoid)
        wp_raw = [load_rows("wp_raw0", wp, 0)]
        tab = [load_table(0)]
        for q in range(4):
            nc.sync.dma_start(
                out=wt_sc_raw[32 * q : 32 * q + 4, :].bitcast(I32).rearrange("r (a w) -> r a w", a=PASSES),
                in_=wt_scales[:, 4 * q : 4 * q + 4, :].bitcast(I32).rearrange("a r w -> r a w"),
            )
        wp_raw.append(load_rows("wp_raw1", wp, 1))
        tab.append(load_table(1))
        wt_raw = tile("wt_raw", [P, PASSES, H // 2], I32, "small")
        nc.sync.dma_start(out=wt_raw[:], in_=wt_words.bitcast(I32).rearrange("a p w -> p a w"))
        wr_raw = [load_rows("wr_raw0", wr, 0)]
        gain = tile("gain", [P, 13], F32, "small", 2 * KIB)
        g_rows = g.rearrange("(c x) -> c x", x=16)
        for i in range(4):
            nc.sync.dma_start(out=gain[i:P:4, :], in_=g_rows[:, i : i + 13])
        wr_raw.append(load_rows("wr_raw1", wr, 1))
        wo_raw = tile("wo_raw", [P, 4, N], F32)
        wo_rows = wo.rearrange("(c t i) n -> t c i n", t=4, i=4)
        for t in range(4):
            nc.sync.dma_start(out=wo_raw[:, t, :], in_=wo_rows[t])

        def gather(name, window, n, s0, count, dtype, place=None, at=0):
            picked = tile(name, [P, count], dtype, place, at)
            nc.vector.tensor_copy(picked[:], window.indirect(lists[n][:, s0 // 16 : (s0 + count) // 16]))
            return picked

        def gather_scales(n, place=None, at=0):
            return gather("sc%d" % n, tab_sc[:], n, 0, S, U8, place, at)

        words = {}

        def pick(n, a, chunk, chunks=1, place=None, at=0):
            picked = gather(
                "w%d_%d_%d" % (n, a, chunk), tab[a][:].bitcast(U32), n, chunk * CHUNK, chunks * CHUNK, U32, place, at
            )
            for c in range(chunks):
                words[n, a, chunk + c] = picked[:, c * CHUNK : (c + 1) * CHUNK]

        def round_on_scalar(grouped, raw, t0, t1):
            dst = grouped[:].rearrange("p (t c i j) -> p t c j i", t=4, i=4, j=4)[:, t0:t1]
            src = raw[:].rearrange("p j (c t i) -> p t c j i", t=4, i=4)
            nc.scalar.copy(out=dst, in_=src[:, t0:t1])

        def round_on_gpsimd(grouped, raw, t0, t1):
            dst = grouped[:].rearrange("p (t c i j) -> p c t i j", t=4, i=4, j=4)[:, :, t0:t1]
            src = raw[:].rearrange("p j (c t i) -> p c t i j", t=4, i=4)
            nc.gpsimd.tensor_scalar(out=dst, in0=src[:, :, t0:t1], scalar1=1.0, scalar2=0.0, op0=MULT, op1=ADD)

        def quantize(name, grouped, width, place=None, at=0):
            codes = tile(name + "_codes", [P, width], U32, place, at)
            scales = tile(name + "_scales", [P, width], U8)
            nc.vector.quantize_mx(out=codes[:].bitcast(FP8X4), scales=scales[:], in_=grouped)
            return codes, scales

        def quantize_slots(name, grouped, width, place=None, at=0):
            codes, scales = quantize(name, grouped, width, place, at)
            return [(codes[:, m : m + P], scales[:, m : m + P]) for m in range(0, width, P)]

        def fp8_pass(dst, t, weight, moving, scales, start, stop):
            nc.tensor.matmul_mx(
                out=dst,
                lhsT=weight[t][0].bitcast(FP8X4),
                lhsT_scale=weight[t][1],
                rhs=moving.bitcast(FP8X4),
                rhs_scale=scales,
                start=start,
                stop=stop,
            )

        wt_sc = tile("wt_sc", [P, PASSES * H // 4], I32)
        wp_bf = [tile("wp_bf0", [P, 4 * H], BF16, "stage", 3 * KIB)]
        wp_q = []
        round_on_scalar(wp_bf[0], wp_raw[0], 0, 4)
        tok_sc0 = gather_scales(TOKEN)
        tok_sc1 = tile("tok_sc1", [P, S], U8)
        nc.gpsimd.dma_start(out=tok_sc1[0:100, :].bitcast(I32), in_=tok_sc0[4:104, :].bitcast(I32))
        nc.gpsimd.tensor_copy(
            out=wt_sc[:].rearrange("p (a t c) -> p a t c", a=PASSES, t=4),
            in_=wt_sc_raw[:].bitcast(I32).rearrange("p (a c t) -> p a t c", a=PASSES, t=4),
        )
        page_sc = gather_scales(PAGE)
        wr_q = []

        def sums(first_bank, width):
            if width == CHUNK:
                return [(bank(first_bank + b), 0, CHUNK, (2 * b, 2 * b + 1)) for b in range(2)]
            return [(bank(first_bank + b), b * UNIT, UNIT, (0, 1, 2, 3)) for b in range(2)]

        def stage_pass(layout, chunk, n, a, first, last):
            for dst, e0, width, slots in layout:
                cols = slice(chunk * CHUNK + e0, chunk * CHUNK + e0 + width)
                moving = words[n, a, chunk][:, e0 : e0 + width]
                for k, t in enumerate(slots):
                    part = dst[:, k * width : (k + 1) * width]
                    start = first and k == 0
                    stop = last and k == len(slots) - 1
                    if n == PAGE:
                        fp8_pass(part, t, wp_q[a], moving, page_sc[4 * a : P, cols], start, stop)
                    elif n == PRED:
                        fp8_pass(part, t, wr_q[a], moving, pred_sc[4 * a : P, cols], start, stop)
                    else:
                        w0 = (4 * a + t) * (P // 2)
                        c0 = (4 * a + t) * (P // 4)
                        nc.tensor.matmul_mx(
                            out=part,
                            lhsT=wt_codes[:, w0 : w0 + P // 2].bitcast(FP4X4),
                            lhsT_scale=wt_sc[:, c0 : c0 + P // 4].bitcast(U8),
                            rhs=moving.bitcast(FP8X4),
                            rhs_scale=(tok_sc0, tok_sc1)[a][:, cols],
                            start=start,
                            stop=stop,
                        )

        def leave(result, c0, layout, func):
            for dst, e0, width, slots in layout:
                nc.scalar.activation(
                    out=result[:, slots[0] : slots[-1] + 1, c0 + e0 : c0 + e0 + width],
                    in_=dst[:].rearrange("p (t e) -> p t e", e=width),
                    func=func,
                )

        def squash(chunk):
            result = tile("cell%d" % chunk, [P, 4, CHUNK], F32)
            leave(result, 0, cell[chunk], ACT.Tanh)
            return result

        def apply_gain(gate, sig, slots):
            for t in slots:
                nc.scalar.activation(out=gate[:, t, :], in_=sig[:, t, :], func=ACT.Copy, scale=gain[:, 4 * t : 4 * t + 1])

        def product(engine, walk, s0, width, place=None):
            h_bf = tile("h_bf%d" % s0, [P, 4 * width], BF16, place)
            gate = gates[s0 // HALF][:, :, s0 % HALF : s0 % HALF + width]
            state = cells[s0 // CHUNK][:, :, s0 % CHUNK : s0 % CHUNK + width]
            engine.tensor_tensor(
                out=h_bf[:].rearrange("p (c i t) -> " + walk, t=4, i=4),
                in0=gate.rearrange("p t (c i) -> " + walk, i=4),
                in1=state.rearrange("p t (c i) -> " + walk, i=4),
                op=MULT,
            )
            return h_bf

        out_rows = out.rearrange("(nt p) s -> p nt s", p=P)

        def project(s0, width, h_bf, state):
            project_codes(s0, 0, width, quantize("h%d" % s0, h_bf[:], width), state)

        def project_codes(s0, c0, width, h_q, state):
            h_codes, h_scales = h_q[0][:, c0:], h_q[1][:, c0:]
            for u0 in range(0, width, UNIT):
                dst = bank((s0 + u0) // UNIT)
                for nt in range(3):
                    fp8_pass(
                        dst[:, nt * UNIT : (nt + 1) * UNIT], nt, wo_q, h_codes[:, u0 : u0 + UNIT],
                        h_scales[:, u0 : u0 + UNIT], True, True,
                    )
                nc.scalar.activation(
                    out=state[:, :, u0 : u0 + UNIT],
                    in_=dst[:, : 3 * UNIT].rearrange("p (nt s) -> p nt s", nt=3),
                    func=ACT.Tanh,
                )

        page = {chunk: sums(2 * chunk, CHUNK) for chunk in (A, B, C, D)}
        pick(PAGE, 0, A, 2)
        wp_q.append(quantize_slots("wp0", wp_bf[0][:], H))
        wp_bf.append(tile("wp_bf1", [P, 4 * H], BF16, "stage", 3 * KIB))
        round_on_scalar(wp_bf[1], wp_raw[1], 2, 4)
        round_on_gpsimd(wp_bf[1], wp_raw[1], 0, 2)
        pick(PAGE, 0, C, 2, "wp_raw0", 0)
        for chunk in (A, B, C, D):
            stage_pass(page[chunk], chunk, PAGE, 0, True, False)
        pick(TOKEN, 0, A, 2, "wp_raw0", 2 * KIB)
        wp_q.append(quantize_slots("wp1", wp_bf[1][:], H))
        wt_codes = tile("wt_codes", [P, PASSES * H // 2], I32, "stage", 5 * KIB)
        nc.gpsimd.tensor_copy(
            out=wt_codes[:].rearrange("p (a t c w) -> p a t c w", a=PASSES, t=4, w=2),
            in_=wt_raw[:].rearrange("p a (c t w) -> p a t c w", t=4, w=2),
        )
        pick(PAGE, 1, A, 2, "wp_raw1", 7 * KIB)
        sigs = [tile("sig0", [P, 4, HALF], F32)]
        for chunk in (A, B):
            stage_pass(page[chunk], chunk, PAGE, 1, False, True)
            leave(sigs[0], chunk * CHUNK, page[chunk], ACT.Sigmoid)
        pick(PAGE, 1, C, 2, "wp_raw1", KIB)
        for chunk in (C, D):
            stage_pass(page[chunk], chunk, PAGE, 1, False, True)
        pred_sc = gather_scales(PRED, "wp_raw1")
        wr_bf = [tile("wr_bf0", [P, 4 * H], BF16, "stage", KIB)]
        round_on_gpsimd(wr_bf[0], wr_raw[0], 0, 4)
        gates = [tile("gate0", [P, 4, HALF], F32)]
        apply_gain(gates[0], sigs[0], (0, 1))
        wr_bf.append(tile("wr_bf1", [P, 4 * H], BF16, "late"))
        round_on_gpsimd(wr_bf[1], wr_raw[1], 0, 2)
        round_on_scalar(wr_bf[1], wr_raw[1], 2, 4)
        apply_gain(gates[0], sigs[0], (2, 3))
        cell = {A: sums(0, CHUNK), B: sums(2, CHUNK)}
        stage_pass(cell[A], A, TOKEN, 0, True, False)
        stage_pass(cell[B], B, TOKEN, 0, True, False)
        pick(PRED, 1, A, 1, "wp_raw1", 3 * KIB)
        pick(TOKEN, 1, A, 1, "wp_raw0", 3 * KIB)
        stage_pass(cell[A], A, TOKEN, 1, False, False)
        pick(PRED, 0, A, 2, "wp_raw0", KIB)
        wr_q.append(quantize_slots("wr0", wr_bf[0][:], H, "wr_raw0", 7 * KIB))
        wr_q.append(quantize_slots("wr1", wr_bf[1][:], H))
        stage_pass(cell[A], A, PRED, 0, False, False)
        stage_pass(cell[A], A, PRED, 1, False, True)
        cells = [squash(A)]
        sigs.append(tile("sig1", [P, 4, HALF], F32, "wr_raw1", 7 * KIB))
        for chunk in (C, D):
            leave(sigs[1], (chunk - C) * CHUNK, page[chunk], ACT.Sigmoid)
        wo_bf = tile("wo_bf", [P, 4 * N], BF16, "late", 2 * KIB)
        nc.gpsimd.tensor_scalar(
            out=wo_bf[:].rearrange("p (n t) -> p n t", t=4)[:, : 2 * P],
            in0=wo_raw[:].rearrange("p t n -> p n t")[:, : 2 * P],
            scalar1=1.0, scalar2=0.0, op0=MULT, op1=ADD,
        )
        gates.append(tile("gate1", [P, 4, HALF], F32))
        made = {0: product(nc.gpsimd, "p c t i", 0, CHUNK)}

        cell[C] = sums(4, CHUNK)
        for k, n in enumerate((TOKEN, PRED)):
            pick(n, 1, B, 2, "wr_raw1", (1 + 2 * k) * KIB)
            stage_pass(cell[B], B, n, 1, False, k == 1)
            if n == TOKEN:
                stage_pass(cell[B], B, PRED, 0, False, False)
            stage_pass(cell[C], C, n, 1, k == 0, False)
        cells.append(squash(B))
        cell[D] = sums(6, UNIT)
        for k, n in enumerate((TOKEN, PRED)):
            pick(n, 0, C, 2, ("wr_raw1", "late")[k], (5 * KIB, 0)[k])
            stage_pass(cell[C], C, n, 0, False, k == 1)
            stage_pass(cell[D], D, n, 0, k == 0, False)
        cells.append(squash(C))
        nc.scalar.copy(
            out=wo_bf[:].rearrange("p (c i t) -> p c t i", t=4, i=4)[:, P // 2 :],
            in_=wo_raw[:].rearrange("p t (c i) -> p c t i", i=4)[:, P // 2 :],
        )
        apply_gain(gates[1], sigs[1], range(4))
        for k, n in enumerate((TOKEN, PRED)):
            pick(n, 1, D, 1, "wp_raw1", 2 * KIB + 512 + k * KIB)
            stage_pass(cell[D], D, n, 1, False, k == 1)

        wo_q = quantize_slots("wo", wo_bf[:], N, "tab0")
        first_q = quantize("h0", made[0][:], CHUNK)
        for s0 in range(0, CHUNK, UNIT):
            state = tile("state%d" % s0, [P, 3, UNIT], F32)
            project_codes(s0, s0, UNIT, first_q, state)
            nc.sync.dma_start(out=out_rows[:, :, s0 : s0 + UNIT], in_=state[:])
        cells.append(squash(D))
        made[CHUNK] = product(nc.vector, "p c t i", CHUNK, CHUNK, "tab1")
        s0 = CHUNK
        for store in STORES:
            first = s0
            state = tile("state%d" % first, [P, 3, sum(store)], F32)
            for width in store:
                if s0 + width < S:
                    made[s0 + width] = product(nc.vector, "p c t i", s0 + width, UNIT)
                project(s0, width, made[s0], state[:, :, s0 - first : s0 - first + width])
                s0 = s0 + width
            queue = nc.sync if s0 < S else nc.scalar
            queue.dma_start(out=out_rows[:, :, first:s0], in_=state[:])
